import numpy as np, ml_dtypes
CORES = [35,38,43,46]
N = 4
BF = ml_dtypes.bfloat16
W, S, PA, TH, E, R = 4096, 256, 2, 136, 12, 5
def near(rng, pro, kin, amp):
    v = pro[np.arange(8)[None, :, None], kin]; v = v + rng.integers(-amp, amp + 1, v.shape)
    return np.ascontiguousarray(np.minimum(np.maximum(v, 0), 255).transpose(0, 1, 3, 2))
def parts(rng, ends=False):
    pro = rng.integers(0, 256, (8, 3, 16))
    x = near(rng, pro, rng.integers(0, 3, (N, 8, S)), E); d = near(rng, pro, rng.integers(0, 3, (N, 8, W)), E)
    d = np.where(rng.random((N, 8, 1, W)) < 0.25, rng.integers(0, 256, d.shape), d)
    key = rng.random((N, 8, R, W))
    if ends: key[..., 0] = -1.0; key[..., W - 1] = -1.0
    a = np.argsort(key, axis=-1)[..., :S]
    a = rng.permuted(a, axis=-1)
    b = rng.integers(0, W, (N, 8, R, S)); o = rng.integers(0, W, (N, 8, 16, S)); k = rng.integers(0, 2 * R, o.shape)
    for r in range(N):
        for t in range(R): o[r] = np.where(k[r] == t, a[(r + t) % N, :, t][:, None, :], o[r])
    h = np.where(rng.random((N, 8, W)) < 0.5, grantors(rng, a, W), rng.integers(0, W, (N, 8, W)))
    return x, d, o, h, a, b
def grantors(rng, a, n):
    return np.take_along_axis(a.reshape(N, 8, R * S), rng.integers(0, R * S, (N, 8, n)), 2)
def pack(x, d, o, h, a, b):
    return {"own": np.ascontiguousarray(o).reshape(N, 128, S).astype(np.int32), "lm": np.ascontiguousarray(x).reshape(N, 128, S).astype(np.float32).astype(BF),
            "bk": np.ascontiguousarray(d).reshape(N, 128, W).astype(np.float32).astype(BF), "heir": np.ascontiguousarray(h).astype(np.int32),
            "da": np.ascontiguousarray(a).reshape(N, 8, R * S).astype(np.int32), "db": np.ascontiguousarray(b).reshape(N, 8, R * S).astype(np.int32)}
def setup_inputs(rng):
    return pack(*parts(rng))
def setup_inputs_ties(rng):
    x, d, o, h, a, b = parts(rng); mid = rng.integers(60, 196, (8, 16)); x = x * 0 + mid[None, :, :, None]
    s = TH + rng.integers(-1, 2, (N, 8, 1, W)); v = s // 16 + (np.arange(16)[None, None, :, None] < s % 16)
    u = rng.integers(0, (TH - 1) // 16 + 1, (N, 8, 8, W)); v[:, :, :8] += u; v[:, :, 8:] -= u
    d = mid[None, :, :, None] + v * (1 - 2 * rng.integers(0, 2, v.shape))
    return pack(x, d, o, h, a, b)
def setup_inputs_wake(rng):
    x, d, o, h, a, b = parts(rng); pro = rng.integers(40, 216, (8, 1, 16))
    x = near(rng, pro, np.zeros((N, 8, S), np.int64), E // 2); d = rng.integers(0, 256, d.shape)
    o1 = grantors(rng, a, 16 * S).reshape(o.shape); o2 = np.roll(grantors(rng, a, 16 * S), -1, axis=0).reshape(o.shape)
    o = np.where(rng.random(o.shape) < 0.6, o1, o2); h = grantors(rng, a, W); b = np.roll(grantors(rng, a, R * S), -1, axis=0).reshape(b.shape)
    return pack(x, d, o, h, a, b)
def setup_inputs_sleep(rng):
    x, d, o, h, a, b = parts(rng); m = rng.permutation(8); g = m[0]
    a[:, g] = 2 * np.argsort(rng.random((N, W // 2)), axis=-1)[:, :R * S].reshape(N, R, S); x[:, g, :, ::8] = 0
    o[:, g] = 2 * rng.integers(0, W // 2, (N, 16, S)) + 1; h[:, g] = 2 * rng.integers(0, W // 2, (N, W)) + 1; b[:, g] = 2 * rng.integers(0, W // 2, (N, R, S)) + 1
    g = m[1]; a[:, g] = np.argsort(rng.random((N, R, S)), axis=-1)
    o[:, g] = rng.integers(S, W, (N, 16, S)); h[:, g] = rng.integers(S, W, (N, W)); b[:, g] = rng.integers(S, W, (N, R, S))
    nxt = np.roll(a, -1, axis=0)
    for g in m[2:4]:
        x[:, g] = rng.integers(155, 256, (N, 16, S)); d[:, g] = rng.integers(0, 101, (N, 16, W)); b[:, g, :R - 1] = nxt[:, g, 1:]
    o[:, m[2]] = a[:, m[2], 0][:, None, :]; o[:, m[3], 15] = a[:, m[3], 0]
    pro = rng.integers(0, 256, (8, 1, 16)); xn = near(rng, pro, np.zeros((N, 8, S), np.int64), E // 4); dn = near(rng, pro, np.zeros((N, 8, W), np.int64), E // 4)
    for g in m[4:6]:
        x[:, g] = xn[:, g]; d[:, g] = dn[:, g]; h[:, g] = (np.arange(W) + 1) % W
    for r in range(N):
        o[r, m[4]] = rng.permutation((W - 1 - np.arange(16 * S)) % W).reshape(16, S)
        o[r, m[5]] = W - 1 - (r % 2) * rng.integers(0, W // 4, (16, S))
    return pack(x, d, o, h, a, b)
def setup_inputs_alike(rng):
    x, d, o, h, a, b = parts(rng, True); c = 255 * rng.integers(0, 2, (8, 16))[None, :, :, None]; q = rng.permutation(N)
    x = x * 0 + c; x[..., 1::2] = 255 - x[..., 1::2]; x[q[0]] = c[0]
    v = np.where(rng.random((N, 8, 1, W)) < 0.5, c, 255 - c); v[q[0]] = c[0]
    two = rng.random((N, 8, 1, W)) < 0.25; two[q[0]] = False
    s = np.where(two, rng.choice(np.array([128, 160]), two.shape), rng.choice(np.array([0, TH, TH, TH + 1, TH + 1, 255]), two.shape))
    s[q[0]] = rng.choice(np.array([0, TH, TH]), (8, 1, W))
    i = rng.integers(0, 16, two.shape); j = (i + rng.choice(np.array([1, 2, 4, 8, 8]), two.shape)) % 16; p = np.arange(16)[None, None, :, None]
    one = (p == i) | (two & (p == j)); d = v + np.where(v == 0, s, -s) * one
    few = np.array([0, W - 1, W // 2, 3]); o[:, ::2] = rng.choice(few, (N, 4, 16, S))
    h = np.where(rng.random(h.shape) < 0.4, rng.choice(few, h.shape), h); b = np.where(rng.random(b.shape) < 0.3, rng.choice(few, b.shape), b)
    b[..., ::16] = a[..., ::16]; o[q[1], :, 5] = a[q[1], :, 0]
    return pack(x, d, o, h, a, b)
def setup_inputs_spread(rng):
    x, d, o, h, a, b = parts(rng); pro = (np.exp2(8 * rng.random((8, 3, 16))) - 1).astype(np.int64)
    x = near(rng, pro, (3 * rng.random((N, 8, S)) ** 2).astype(np.int64), rng.integers(0, 2 * E + 1, (N, 8, S, 1)))
    d = near(rng, pro, (3 * rng.random((N, 8, W)) ** 2).astype(np.int64), rng.integers(0, 2 * E + 1, (N, 8, W, 1)))
    o = np.where(rng.random(o.shape) < 0.5, (W * rng.random(o.shape) ** 3).astype(np.int64), o)
    h = (W * rng.random(h.shape) ** 3).astype(np.int64); b = (W * rng.random(b.shape) ** 3).astype(np.int64)
    return pack(x, d, np.minimum(o, W - 1), np.minimum(h, W - 1), a, np.minimum(b, W - 1))
def check_inputs(d):
    bad = []
    for k in ("own", "heir", "da", "db"):
        if np.min(d[k]) < 0 or np.max(d[k]) > W - 1: bad.append("range of " + k)
    for k in ("lm", "bk"):
        v = np.asarray(d[k]).astype(np.float32)
        if not np.all((v >= 0) & (v <= 255) & (v == np.floor(v))): bad.append("whole numbers from 0 to 255 in " + k)
    s = np.sort(np.asarray(d["da"]).reshape(N, 8, R, S), axis=-1)
    if np.any(s[..., 1:] == s[..., :-1]): bad.append("different grantors in a round of a rank and group")
    return bad
def reference(own, lm, bk, heir, da, db):
    o = own.astype(np.int64).reshape(N, 8, 16, S); x = lm.astype(np.float32).astype(np.int32).reshape(N, 8, 16, S)
    d = bk.astype(np.float32).astype(np.int32).reshape(N, 8, 16, W); h = heir.astype(np.int64)
    for t in range(R):
        for r in range(N):
            c = (r + t) % N
            a = da[c][:, t * S:(t + 1) * S].astype(np.int64); b = db[c][:, t * S:(t + 1) * S].astype(np.int64)
            hit = o[r] == a[:, None, :]
            o[r] = np.where(hit, b[:, None, :], o[r])
            g, i = np.nonzero(~np.any(hit, axis=1))
            d[c][g, :, a[g, i]] = x[r][g, :, i]
            h[c][g, a[g, i]] = b[g, i]
            for s in range(PA):
                e = o[r].reshape(8, 16 * S)
                w = np.take_along_axis(d[c], e[:, None, :], 2).reshape(8, 16, 16, S)
                dist = np.add.reduce(np.abs(w - x[r][:, :, None, :]), axis=1)
                o[r] = np.where(dist <= TH, np.take_along_axis(h[c], e, 1).reshape(8, 16, S), o[r])
    return {"yo": o.reshape(N, 128, S).astype(np.float32), "yd": d.reshape(N, 128, W).astype(np.float32).astype(BF), "yh": h.astype(np.float32)}

@@ -1,0 +1,479 @@
+from concourse.mybir import AluOpType as A, ActivationFunctionType as F
+
+BIAS = 2048
+TH = 136.5
+R = 5
+
+SCRATCH = {}
+SEMAPHORES = ["v", "s", "t", "p", "loc", "dout"]
+
+
+def _buf(name, cols, dtype, where="sbuf", rows=128):
+    SCRATCH[name] = (where, [rows, cols], dtype)
+
+
+for _n, _c in (("pi", 1), ("ci", 128), ("p15i", 1), ("p4i", 1), ("oddi", 1), ("c15i", 128), ("c4i", 128), ("chi", 128),
+               ("ownI", 256), ("heirI", 256)):
+    _buf(_n, _c, "int32")
+_buf("daI", 1280, "int32", rows=8)
+_buf("dbI", 1280, "int32", rows=8)
+for _n in ("pf", "p15", "p4", "p16", "odd", "l01", "l03", "l23", "m13"):
+    _buf(_n, 1, "float32")
+for _n, _c in (("BO", 128), ("nBO", 128), ("maskP", 128), ("C01", 128), ("C23", 128), ("WN", 128), ("B01", 128),
+               ("Z2", 128), ("RM", 8), ("RH", 24), ("K4", 8), ("Z3", 128), ("C16", 128), ("WY", 2048),
+               ("W", 8192), ("HN", 8192), ("M0", 2048), ("M1", 2048), ("H0", 2048), ("H1", 2048), ("Yx0", 512), ("Yx1", 512),
+               ("Yn", 256), ("NH0", 256), ("NH1", 256), ("HT0", 128), ("HT1", 128), ("X0", 128), ("X1", 128),
+               ("SG0", 128), ("SG1", 128), ("lm0", 256), ("lm1", 256), ("lm2", 256), ("lm3", 256),
+               ("lr0", 4096), ("lr1", 4096), ("lr2", 4096), ("lr3", 4096)):
+    _buf(_n, _c, "bfloat16")
+for _n, _c in (("IdH", 128), ("HI2", 256), ("WH", 2048), ("K1", 8), ("Hs", 256), ("ownH", 256), ("ownN0", 128), ("ownN1", 128),
+               ("OT0", 128), ("OT1", 128), ("MA0", 256), ("MA1", 256)):
+    _buf(_n, _c, "float16")
+for _n, _c in (("E8", 128), ("nE8", 128), ("E01", 128), ("ab", 1280), ("bb", 1280)):
+    _buf(_n, _c, "float16", rows=8)
+for _n, _c in (("AN", 1280), ("BA", 1280), ("hb0", 128), ("hb1", 128), ("tt0", 128), ("tt1", 128), ("yof", 256), ("yhf", 256)):
+    _buf(_n, _c, "float32")
+_buf("off", 256, "uint16")
+_buf("LS0", 8, "uint16")
+_buf("LS1", 8, "uint16")
+for _t in range(4):
+    for _c in range(2):
+        _buf("SD%d%d" % (_t, _c), 128, "float16")
+        _buf("R%d%d" % (_t + 1, _c), 128, "float16")
+        SEMAPHORES.append("r%d%d" % (_t + 1, _c))
+for _t in (1, 2, 3):
+    SEMAPHORES.append("l%d" % _t)
+for _n in ("own", "lm", "heir", "da", "db", "bk0", "bk1", "bk2", "bk3"):
+    SEMAPHORES.append("d_" + _n)
+for _k in range(8):
+    _buf("b%d" % _k, 512, "float32", "psum")
+BANKS = ["b%d" % _k for _k in range(8)]
+
+
+def rank_program(g, core, T, topo):
+    rank = T.rank_of(core)
+    if rank is None:
+        return
+    n = len(T.cores)
+    eng = {"v": g.vector, "s": g.scalar, "t": g.tensor, "p": g, "y": g.sync}
+    know = {q: {} for q in eng}
+    cnt = {}
+    snap = {}
+    wr, rd, acc = {}, {}, {}
+
+    def wait(q, deps):
+        todo = {s: c for s, c in deps.items() if know[q].get(s, 0) < c}
+        for s, c in sorted(todo.items()):
+            if any(o != s and snap.get((o, oc), {}).get(s, 0) >= c for o, oc in todo.items()):
+                continue
+            eng[q].wait_ge(T.sem[s], c)
+        for s, c in todo.items():
+            for s2, c2 in snap.get((s, c), {}).items():
+                know[q][s2] = max(know[q].get(s2, 0), c2)
+            know[q][s] = max(know[q].get(s, 0), c)
+
+    def deps_of(q, reads, writes):
+        d = {}
+
+        def put(src, skip=None):
+            for s, c in src.items():
+                if s != skip:
+                    d[s] = max(d.get(s, 0), c)
+        for k in list(reads) + list(writes):
+            if k in BANKS:
+                put(acc.get(k, {}), q)
+            else:
+                put(wr.get(k, {}))
+        for k in writes:
+            if k not in BANKS:
+                put(rd.get(k, {}))
+        return d
+
+    def note(q, sem, inc, reads, writes):
+        cnt[sem] = cnt.get(sem, 0) + inc
+        c = cnt[sem]
+        snap[(sem, c)] = dict(know[q])
+        for k in list(reads) + list(writes):
+            if k in BANKS:
+                acc.setdefault(k, {})[sem] = c
+        for k in reads:
+            if k not in BANKS:
+                rd.setdefault(k, {})[sem] = c
+        for k in writes:
+            if k not in BANKS:
+                wr[k] = {sem: c}
+                rd[k] = {}
+
+    def op(q, fn, reads, writes, sem=None, inc=1):
+        wait(q, deps_of(q, reads, writes))
+        sem = sem or q
+        fn().then_inc(T.sem[sem], inc)
+        note(q, sem, inc, reads, writes)
+
+    def ts(out, in0, s1, op0, reads, writes, s2=None, op1=None):
+        if op1 is None:
+            op("v", lambda: g.vector.tensor_scalar(out=out, in0=in0, scalar1=s1, scalar2=None, op0=op0), reads, writes)
+        else:
+            op("v", lambda: g.vector.tensor_scalar(out=out, in0=in0, scalar1=s1, scalar2=s2, op0=op0, op1=op1), reads, writes)
+
+    def tt(out, in0, in1, o, reads, writes):
+        op("v", lambda: g.vector.tensor_tensor(out=out, in0=in0, in1=in1, op=o), reads, writes)
+
+    def vcopy(out, in_, reads, writes):
+        op("v", lambda: g.vector.tensor_copy(out=out, in_=in_), reads, writes)
+
+    def act(out, in_, reads, writes, func=F.Copy, **kw):
+        op("s", lambda: g.scalar.activation(out=out, in_=in_, func=func, **kw), reads, writes)
+
+    def mm(out, lhsT, rhs, start, stop, reads, writes):
+        op("t", lambda: g.tensor.matmul(out=out, lhsT=lhsT, rhs=rhs, start=start, stop=stop), reads, writes)
+
+    def load(q, out, in_, sem, key):
+        op(q, lambda: eng[q].dma_start(out=out, in_=in_), [], [key], sem, 16)
+
+    b = [T[k] for k in BANKS]
+
+    load("y", T.lm0[:], T.lm[:], "d_lm", "lm0")
+    load("y", T.daI[:], T.da[:], "d_da", "daI")
+    for k in range(4):
+        load("s", T.W[:, 1024 * k:1024 * k + 1024], T.bk[:, 1024 * k:1024 * k + 1024], "d_bk%d" % k, "Wk%d" % k)
+    load("y", T.dbI[:], T.db[:], "d_db", "dbI")
+    load("y", T.ownI[:], T.own[:], "d_own", "ownI")
+    load("y", T.heirI[:], T.heir[:], "d_heir", "heirI")
+    WK = ["Wk%d" % k for k in range(4)]
+    HK = ["HN%d" % k for k in range(8)]
+
+    op("p", lambda: g.iota(T.pi[:], [[0, 1]], 0, 1), [], ["pi"])
+    op("p", lambda: g.iota(T.ci[:], [[1, 128]], 0, 0), [], ["ci"])
+
+    def send(dst, out, in_, sem, key):
+        wait("p", deps_of("p", [key], []))
+        rid, pid, _ = topo.addr(dst)
+        ne = len(topo.engines(core, dst))
+        g.remote_dma(out, in_, T.sem[sem], T.sem.loc, pid, rid, topo.mask(core, dst))
+        cnt["loc"] = cnt.get("loc", 0) + ne
+
+    def arrive(sem, key, src):
+        ne = len(topo.engines(src, core))
+        cnt[sem] = ne
+        wr[key] = {sem: ne}
+        rd[key] = {}
+
+    for t in (1, 2, 3):
+        send(T.cores[(rank + t) % n], T["lm%d" % t][:], T.lm0[:], "l%d" % t, "lm0")
+        arrive("l%d" % t, "lm%d" % t, T.cores[(rank - t) % n])
+
+    def bits(out, in0, s1, op0, reads, writes, s2=None, op1=None):
+        ts(out, in0, s1, op0, reads, writes, s2, op1)
+
+    bits(T.p15i[:], T.pi[:], 15, A.bitwise_and, ["pi"], ["p15i"])
+    bits(T.p4i[:], T.pi[:], 4, A.arith_shift_right, ["pi"], ["p4i"])
+    bits(T.oddi[:], T.pi[:], 1, A.bitwise_and, ["pi"], ["oddi"])
+    vcopy(T.pf[:], T.pi[:], ["pi"], ["pf"])
+    bits(T.c4i[:], T.ci[:], 4, A.arith_shift_right, ["ci"], ["c4i"])
+    bits(T.c15i[:], T.ci[:], 15, A.bitwise_and, ["ci"], ["c15i"])
+    bits(T.chi[:], T.ci[:], 1, A.arith_shift_right, ["ci"], ["chi"], 7, A.bitwise_and)
+    vcopy(T.p15[:], T.p15i[:], ["p15i"], ["p15"])
+    vcopy(T.p4[:], T.p4i[:], ["p4i"], ["p4"])
+    vcopy(T.odd[:], T.oddi[:], ["oddi"], ["odd"])
+    ts(T.E8[:], T.c4i[0:8, :], T.pf[0:8, :], A.is_equal, ["c4i", "pf"], ["E8"])
+    ts(T.ab[:, 0:256], T.daI[:, 0:256], BIAS, A.subtract, ["daI"], ["ab0"])
+    ts(T.C01[:], T.chi[:], 0, A.is_equal, ["chi"], ["C01"])
+    ts(T.C23[:], T.chi[:], 1, A.is_equal, ["chi"], ["C23"])
+    ts(T.BO[:], T.c4i[:], T.p4[:], A.is_equal, ["c4i", "p4"], ["BO"])
+    ts(T.maskP[:], T.c15i[:], T.p15[:], A.is_equal, ["c15i", "p15"], ["maskP"])
+    ts(T.nE8[:], T.E8[:], -1.0, A.mult, ["E8"], ["nE8"])
+    tt(T.E01[:], T.E8[:], T.C01[0:8, :], A.mult, ["E8", "C01"], ["E01"])
+    ts(T.bb[:, 0:256], T.dbI[:, 0:256], BIAS, A.subtract, ["dbI"], ["bb0"])
+    tt(T.WN[:], T.BO[:], T.C23[:], A.mult, ["BO", "C23"], ["WN"])
+    tt(T.B01[:], T.BO[:], T.C01[:], A.mult, ["BO", "C01"], ["B01"])
+    ts(T.l01[:], T.p15[:], 1.0, A.is_le, ["p15"], ["l01"])
+    ts(T.l03[:], T.p15[:], 3.0, A.is_le, ["p15"], ["l03"])
+    ts(T.p16[:], T.p15[:], 1.0, A.add, ["p15"], ["p16"])
+    tt(T.l23[:], T.l03[:], T.l01[:], A.subtract, ["l03", "l01"], ["l23"])
+    tt(T.m13[:], T.l03[:], T.odd[:], A.mult, ["l03", "odd"], ["m13"])
+    ts(T.Z2[:], T.B01[:], T.p16[:], A.mult, ["B01", "p16"], ["Z2"], 1.0, A.subtract)
+    ts(T.ownH[:], T.ownI[:], BIAS, A.subtract, ["ownI"], ["ownH"])
+
+    AR = [(0, 256), (256, 768), (768, 1280)]
+
+    def rng(t):
+        return 0 if t == 0 else 1 if t < 3 else 2
+
+    def build_an(k):
+        lo, hi = AR[k]
+        w = hi - lo
+        kk = "0" if k == 0 else "1"
+        mm(b[0][:, 0:w], T.E8[:], T.ab[:, lo:hi], True, True, ["E8", "ab" + kk], ["b0"])
+        act(T.AN[:, lo:hi], b[0][:, 0:w], ["b0"], ["AN%d" % k])
+        mm(b[1][:, 0:w], T.E8[:], T.bb[:, lo:hi], True, False, ["E8", "bb" + kk], ["b1"])
+        mm(b[1][:, 0:w], T.nE8[:], T.ab[:, lo:hi], False, True, ["nE8", "ab" + kk], ["b1"])
+        act(T.BA[:, lo:hi], b[1][:, 0:w], ["b1"], ["BA%d" % k])
+
+    build_an(0)
+
+    def prep_t(t):
+        kk = "0" if t == 0 else "1"
+        lk = "lm%d" % (t % n)
+        mm(b[7][:, 0:256], T.WN[:], T[lk][:], True, False, ["WN", lk], ["b7"])
+        mm(b[7][:, 0:256], T.E01[:], T.bb[:, 256 * t:256 * t + 256], False, True, ["E01", "bb" + kk], ["b7"])
+        for ch in range(2):
+            mm(b[7][:, 256 + 128 * ch:384 + 128 * ch], T.ab[:, 256 * t + 128 * ch:256 * t + 128 * ch + 128], T.E8[:], True, True,
+               ["ab" + kk, "E8"], ["b7"])
+
+    def prep_s(t):
+        act(T.Yn[:], b[7][:, 0:256], ["b7", "m13"], ["Yn"], scale=T.m13[:])
+
+    def prep_nh(t):
+        tt(T["NH%d" % (t % 2)][:], b[7][:, 0:256], T.Yn[:], A.subtract, ["b7", "Yn"], ["NH%d" % (t % 2)])
+
+    def prep_ma(t):
+        k = "MA%d" % (t % 2)
+        for ch in range(2):
+            tt(T[k][:, 128 * ch:128 * ch + 128], b[7][:, 256 + 128 * ch:384 + 128 * ch], T.maskP[:], A.mult, ["b7", "maskP"], [k + "c%d" % ch])
+
+    def rep(t, q, who):
+        k = "lm%d" % t
+        if who == "v":
+            vcopy(T["lr%d" % t][:, q:4096:16], T[k][:], [k], ["lr%d_%d" % (t, q)])
+        else:
+            act(T["lr%d" % t][:, q:4096:16], T[k][:], [k], ["lr%d_%d" % (t, q)])
+
+    prep_t(0)
+    prep_s(0)
+    ts(T.K1[:], T.BO[:, 0:128:16], 1.0, A.mult, ["BO"], ["K1"])
+    ts(T.K4[:], T.BO[:, 0:128:16], 4096.0, A.mult, ["BO"], ["K4"])
+    prep_ma(0)
+    prep_nh(0)
+    for q in range(10):
+        rep(0, q, "s")
+
+    def deeds(t, ch):
+        c = str(ch)
+        k = str(rng(t))
+        cols = slice(256 * t + 128 * ch, 256 * t + 128 * ch + 128)
+        loc = slice(128 * ch, 128 * ch + 128)
+        if t == 0:
+            own, ok = T.ownH[:, loc], "ownH"
+        else:
+            rk = "R%d%d" % (t, ch)
+            mm(b[2 + ch][:, 0:128], T[rk][:], T.IdH[:], True, True, [rk, "IdH"], ["b%d" % (2 + ch)])
+            own, ok = b[2 + ch][:, 0:128], "b%d" % (2 + ch)
+        tt(T["HT" + c][:], own, T.AN[:, cols], A.is_equal, [ok, "AN" + k], ["HT" + c])
+        mm(b[5 + ch][:, 0:128], T["HT" + c][:], T.BO[:], True, True, ["HT" + c, "BO"], ["b%d" % (5 + ch)])
+        tt(T["hb" + c][:], T["HT" + c][:], T.BA[:, cols], A.mult, ["HT" + c, "BA" + k], ["hb" + c])
+        tt(T["X" + c][:], b[5 + ch][:, 0:128], T.maskP[:], A.min, ["b%d" % (5 + ch), "maskP"], ["X" + c])
+        m = "MA%d" % (t % 2)
+        lst = b[4][:, 8 * ch:8 * ch + 8]
+        mm(lst, T[m][:, loc], T.K1[:], True, False, [m + "c" + c, "K1"], ["b4"])
+        mm(lst, T["X" + c][:], T.K4[:], False, True, ["X" + c, "K4"], ["b4"])
+        tt(T["ownN" + c][:], own, T["hb" + c][:], A.add, [ok, "hb" + c], ["ownN" + c])
+        ts(T["LS" + c][:], lst, BIAS, A.add, ["b4"], ["LS" + c])
+
+    def scatters(t, ch):
+        c = str(ch)
+        h = "NH%d" % (t % 2)
+        l = "lm%d" % (t % n)
+        loc = slice(128 * ch, 128 * ch + 128)
+        vcopy(T.HN[:, 0:8192].indirect(T["LS" + c][:, 0:8]), T[h][:, loc], ["LS" + c, h], HK)
+        vcopy(T.W[:, 0:8192].indirect(T["LS" + c][:, 0:8]), T[l][:, loc], ["LS" + c, l], WK)
+
+    def offs(ch):
+        ts(T.off[:, 128 * ch:128 * ch + 128], T["ownN%d" % ch][:], BIAS, A.add, ["ownN%d" % ch], ["off%d" % ch])
+
+    def gv(t, ch, lo, hi):
+        a, z = 128 * ch + lo, 128 * ch + hi
+        m, l = "M%d" % ch, "lr%d" % (t % n)
+        op("v", lambda: g.vector.tensor_tensor(out=T[m][:, 16 * lo:16 * hi], in0=T.W[:, 0:4096].indirect(T.off[:, a:z]),
+                                               in1=T[l][:, 16 * a:16 * z], op=A.max),
+           WK + ["off%d" % ch] + [l + "_%d" % q for q in range(16)], [m + "_%d" % lo])
+
+    def gs(ch, lo, hi):
+        a, z = 128 * ch + lo, 128 * ch + hi
+        act(T["H%d" % ch][:, 16 * lo:16 * hi], T.HN[:, 0:4096].indirect(T.off[:, a:z]), HK + ["off%d" % ch], ["H%d_%d" % (ch, lo)])
+
+    VS, SS = 96, 64
+    MK = {c: ["M%d_0" % c, "M%d_%d" % (c, VS)] for c in (0, 1)}
+    HHK = {c: ["H%d_0" % c, "H%d_%d" % (c, SS)] for c in (0, 1)}
+
+    def gv_whole(t, ch):
+        gv(t, ch, 0, 128)
+        wr[MK[ch][1]] = dict(wr[MK[ch][0]])
+
+    def gs_whole(ch):
+        gs(ch, 0, 128)
+        wr[HHK[ch][1]] = dict(wr[HHK[ch][0]])
+
+    def init(t, ch, p):
+        l, bk = "lm%d" % (t % n), "b%d" % ch
+        mm(b[ch][:, 0:128], T[l][:, 128 * ch:128 * ch + 128], T.nBO[:], True, False, [l, "nBO"], [bk])
+        if p == 0:
+            mm(b[ch][:, 128:384], T["ownN%d" % ch][:], T.HI2[:], False, False, ["ownN%d" % ch, "HI2"], [bk])
+        else:
+            for k in (1, 2):
+                mm(b[ch][:, 128 * k:128 * k + 128], T.HI2[:, 0:128], T["OT%d" % ch][:], False, False, ["HI2", "OT%d" % ch], [bk])
+
+    def hmm(ch):
+        for q in range(16):
+            mm(b[ch][:, q:384:16], T["H%d" % ch][:, q:2048:16], T.RH[:], False, False, HHK[ch] + ["RH"], ["b%d" % ch])
+
+    def mmm(ch):
+        for q in range(16):
+            mm(b[ch][:, q:128:16], T["M%d" % ch][:, q:2048:16], T.RM[:], False, q == 15, MK[ch] + ["RM"], ["b%d" % ch])
+
+    def sign(ch):
+        act(T["SG%d" % ch][:], b[ch][:, 0:128], ["b%d" % ch], ["SG%d" % ch], func=F.Sign, bias=-TH)
+
+    def upd(ch, dst):
+        c = str(ch)
+        tt(T["tt" + c][:], T["SG" + c][:], b[ch][:, 128:256], A.mult, ["SG" + c, "b" + c], ["tt" + c])
+        tt(T[dst][:], b[ch][:, 256:384], T["tt" + c][:], A.add, ["b" + c, "tt" + c], [dst])
+
+    def turn(ch, src):
+        mm(b[2 + ch][:, 0:128], T[src][:], T.IdH[:], True, True, [src, "IdH"], ["b%d" % (2 + ch)])
+
+    def conv(ch):
+        ts(T.off[:, 128 * ch:128 * ch + 128], b[2 + ch][:, 0:128], BIAS, A.add, ["b%d" % (2 + ch)], ["off%d" % ch])
+
+    deeds(0, 0)
+    deeds(0, 1)
+    ts(T.Hs[:], T.heirI[:], BIAS, A.subtract, ["heirI"], ["Hs"])
+    for k in range(16):
+        ts(T.WH[:, 128 * k:128 * k + 128], T.Z2[:], float(k), A.is_equal, ["Z2"], ["WH%d" % k])
+    offs(0)
+    offs(1)
+    ts(T.nBO[:], T.BO[:], -1.0, A.mult, ["BO"], ["nBO"])
+    ts(T.HI2[:, 0:128], T.ci[:], T.pf[:], A.is_equal, ["ci", "pf"], ["HI2"], 0.5, A.mult)
+    ts(T.HI2[:, 128:256], T.ci[:], T.pf[:], A.is_equal, ["ci", "pf"], ["HI2"], 0.5, A.mult)
+    ts(T.RM[:], T.BO[:, 0:128:16], 2.0, A.mult, ["BO"], ["RM"])
+    ts(T.RH[:, 0:8], T.BO[:, 0:128:16], T.l23[:], A.mult, ["BO", "l23"], ["RH"], -1.0, A.mult)
+    ts(T.RH[:, 8:16], T.BO[:, 0:128:16], T.l01[:], A.mult, ["BO", "l01"], ["RH"], -0.5, A.mult)
+    ts(T.RH[:, 16:24], T.BO[:, 0:128:16], T.l01[:], A.mult, ["BO", "l01"], ["RH"], 0.5, A.mult)
+    for q in range(10, 16):
+        rep(0, q, "v")
+    ts(T.IdH[:], T.ci[:], T.pf[:], A.is_equal, ["ci", "pf"], ["IdH"])
+    ts(T.ab[:, 256:1280], T.daI[:, 256:1280], BIAS, A.subtract, ["daI"], ["ab1"])
+    ts(T.bb[:, 256:1280], T.dbI[:, 256:1280], BIAS, A.subtract, ["dbI"], ["bb1"])
+    build_an(1)
+    build_an(2)
+    XB = (0, 1, 7)
+    for k in range(8):
+        x = XB[k % 3]
+        bk = "b%d" % x
+        y = "Yx%d" % (k % 2)
+        mm(b[x][:], T.WN[:], T.W[:, 512 * k:512 * k + 512], True, False, ["WN", "Wk%d" % (k // 2)], [bk])
+        for j in range(2):
+            w = 2 * k + j
+            mm(b[x][:, 256 * j:256 * j + 256], T.WH[:, 128 * w:128 * w + 128], T.Hs[:], False, j == 1, ["WH%d" % w, "Hs"], [bk])
+        act(T[y][:], b[x][:], [bk, "m13"], [y], scale=T.m13[:])
+        tt(T.HN[:, 512 * k:512 * k + 512], b[x][:], T[y][:], A.subtract, [bk, y], ["HN%d" % k])
+    scatters(0, 0)
+    scatters(0, 1)
+
+    nxt = T.cores[(rank + 1) % n]
+    prv = T.cores[(rank - 1) % n]
+    for t in range(1, R):
+        for ch in range(2):
+            arrive("r%d%d" % (t, ch), "R%d%d" % (t, ch), prv)
+
+    def yh_part(ks):
+        for k in ks:
+            mm(b[4][:, 0:256], T.WY[:, 128 * k:128 * k + 128], T.HN[:, 256 * k:256 * k + 256], k == 0, k == 15,
+               ["WY%d" % k] + HK, ["b4"])
+
+    for t in range(R):
+        last = t == R - 1
+        if t:
+            deeds(t, 0)
+            offs(0)
+            scatters(t, 0)
+            deeds(t, 1)
+            scatters(t, 1)
+            offs(1)
+        init(t, 0, 0)
+        init(t, 1, 0)
+        gv_whole(t, 0)
+        gs_whole(0)
+        if last:
+            op("y", lambda: g.sync.dma_start(out=T.yd[:], in_=T.W[:, 0:4096]), WK, [], "dout", 16)
+            yh_part(range(0, 8))
+        hmm(0)
+        mmm(0)
+        gv(t, 1, 0, VS)
+        gs(1, 0, SS)
+        sign(0)
+        gs(1, SS, 128)
+        upd(0, "OT0")
+        turn(0, "OT0")
+        init(t, 0, 1)
+        if last:
+            yh_part(range(8, 12))
+        else:
+            prep_t(t + 1)
+        gv(t, 1, VS, 128)
+        conv(0)
+        hmm(1)
+        mmm(1)
+        gv(t, 0, 0, VS)
+        gs(0, 0, SS)
+        sign(1)
+        gs(0, SS, 128)
+        upd(1, "OT1")
+        turn(1, "OT1")
+        init(t, 1, 1)
+        if last:
+            yh_part(range(12, 16))
+        gv(t, 0, VS, 128)
+        conv(1)
+        hmm(0)
+        mmm(0)
+        gv(t, 1, 0, VS)
+        gs(1, 0, SS)
+        sign(0)
+        gs(1, SS, 128)
+        if not last:
+            upd(0, "SD%d0" % t)
+            send(nxt, T["R%d0" % (t + 1)][:], T["SD%d0" % t][:], "r%d0" % (t + 1), "SD%d0" % t)
+            gv(t, 1, VS, 128)
+            prep_s(t + 1)
+            hmm(1)
+            mmm(1)
+            prep_ma(t + 1)
+            if t + 1 < n:
+                for q in range(12, 16):
+                    rep(t + 1, q, "v")
+            sign(1)
+            upd(1, "SD%d1" % t)
+            send(nxt, T["R%d1" % (t + 1)][:], T["SD%d1" % t][:], "r%d1" % (t + 1), "SD%d1" % t)
+            prep_nh(t + 1)
+            if t + 1 < n:
+                for q in range(12):
+                    rep(t + 1, q, "s")
+            if t == R - 2:
+                vcopy(T.C16[:], T.c15i[:], ["c15i"], ["C16"])
+                ts(T.C16[:], T.C16[:], 1.0, A.add, ["C16"], ["C16"])
+                tt(T.C16[:], T.C16[:], T.BO[:], A.mult, ["C16", "BO"], ["C16"])
+                ts(T.Z3[:], T.C16[:], T.l01[:], A.mult, ["C16", "l01"], ["Z3"], 1.0, A.subtract)
+                for k in range(16):
+                    ts(T.WY[:, 128 * k:128 * k + 128], T.Z3[:], float(k), A.is_equal, ["Z3"], ["WY%d" % k])
+        else:
+            upd(0, "OT0")
+            turn(0, "OT0")
+            gv(t, 1, VS, 128)
+
+            def out_yo(ch):
+                loc = slice(128 * ch, 128 * ch + 128)
+                ts(T.yof[:, loc], b[2 + ch][:, 0:128], float(BIAS), A.add, ["b%d" % (2 + ch)], ["yof%d" % ch])
+                op("y", lambda: g.sync.dma_start(out=T.yo[:, loc], in_=T.yof[:, loc]), ["yof%d" % ch], [], "dout", 16)
+            hmm(1)
+            mmm(1)
+            ts(T.yhf[:], b[4][:, 0:256], float(BIAS), A.add, ["b4"], ["yhf"])
+            op("y", lambda: g.sync.dma_start(out=T.yh[:], in_=T.yhf[:]), ["yhf"], [], "dout", 16)
+            out_yo(0)
+            sign(1)
+            upd(1, "OT1")
+            turn(1, "OT1")
+            out_yo(1)
+
+    g.sync.wait_ge(T.sem.dout, cnt["dout"])
+    wait("p", {s: c for s, c in cnt.items() if s != "dout"})

@@ -1,8 +1,11 @@
 from concourse.mybir import AluOpType as A, ActivationFunctionType as F
 
 BIAS = 2048
-TH = 136.5
+TH = 136.5 + 2048
 R = 5
+VS, SS = 104, 88
+VR0, VR = 2, 3
+VCOPY = (1, 4, 6)
 
 SCRATCH = {}
 SEMAPHORES = ["v", "s", "t", "p", "loc", "dout"]
@@ -12,26 +15,27 @@ def _buf(name, cols, dtype, where="sbuf", rows=128):
     SCRATCH[name] = (where, [rows, cols], dtype)
 
 
-for _n, _c in (("pi", 1), ("ci", 128), ("p15i", 1), ("p4i", 1), ("oddi", 1), ("c15i", 128), ("c4i", 128), ("chi", 128),
-               ("ownI", 256), ("heirI", 256)):
+for _n, _c in (("pi", 1), ("ci", 128), ("p15i", 1), ("p4i", 1), ("p2i", 1), ("pki", 1), ("pgi", 1), ("phi", 1),
+               ("c15i", 128), ("c4i", 128), ("ownI", 256), ("heirI", 512), ("hcut", 512)):
     _buf(_n, _c, "int32")
 _buf("daI", 1280, "int32", rows=8)
 _buf("dbI", 1280, "int32", rows=8)
-for _n in ("pf", "p15", "p4", "p16", "odd", "l01", "l03", "l23", "m13"):
+for _n in ("pf", "p15", "p4", "p2", "pk", "pg", "ph", "tn", "th", "hb2", "l01", "l29", "m1", "cb", "ncb"):
     _buf(_n, 1, "float32")
-for _n, _c in (("BO", 128), ("nBO", 128), ("maskP", 128), ("C01", 128), ("C23", 128), ("WN", 128), ("B01", 128),
-               ("Z2", 128), ("RM", 8), ("RH", 24), ("K4", 8), ("Z3", 128), ("C16", 128), ("WY", 2048),
-               ("W", 8192), ("HN", 8192), ("M0", 2048), ("M1", 2048), ("H0", 2048), ("H1", 2048), ("Yx0", 512), ("Yx1", 512),
+for _n, _c in (("BO", 128), ("nBO", 128), ("maskP", 128), ("C01", 128), ("WN", 128), ("Z2", 128),
+               ("RM", 8), ("RH", 24), ("K4", 8), ("yha", 256), ("yhb", 256),
+               ("W", 8192), ("HN", 8192), ("M0", 2048), ("M1", 2048), ("H0", 2048), ("H1", 2048),
                ("Yn", 256), ("NH0", 256), ("NH1", 256), ("HT0", 128), ("HT1", 128), ("X0", 128), ("X1", 128),
                ("SG0", 128), ("SG1", 128), ("lm0", 256), ("lm1", 256), ("lm2", 256), ("lm3", 256),
                ("lr0", 4096), ("lr1", 4096), ("lr2", 4096), ("lr3", 4096)):
     _buf(_n, _c, "bfloat16")
-for _n, _c in (("IdH", 128), ("HI2", 256), ("WH", 2048), ("K1", 8), ("Hs", 256), ("ownH", 256), ("ownN0", 128), ("ownN1", 128),
+for _n, _c in (("IdH", 128), ("HI2", 256), ("WH", 1024), ("K1", 8), ("Hs", 512), ("ownH", 256), ("ownN0", 128), ("ownN1", 128),
                ("OT0", 128), ("OT1", 128), ("MA0", 256), ("MA1", 256)):
     _buf(_n, _c, "float16")
 for _n, _c in (("E8", 128), ("nE8", 128), ("E01", 128), ("ab", 1280), ("bb", 1280)):
     _buf(_n, _c, "float16", rows=8)
-for _n, _c in (("AN", 1280), ("BA", 1280), ("hb0", 128), ("hb1", 128), ("tt0", 128), ("tt1", 128), ("yof", 256), ("yhf", 256)):
+for _n, _c in (("AN", 1280), ("BA", 1280), ("hb0", 128), ("hb1", 128), ("tt0", 128), ("tt1", 128),
+               ("yof", 256), ("yh2", 256), ("yhf", 256)):
     _buf(_n, _c, "float32")
 _buf("off", 256, "uint16")
 _buf("LS0", 8, "uint16")
@@ -43,7 +47,7 @@ for _t in range(4):
         SEMAPHORES.append("r%d%d" % (_t + 1, _c))
 for _t in (1, 2, 3):
     SEMAPHORES.append("l%d" % _t)
-for _n in ("own", "lm", "heir", "da", "db", "bk0", "bk1", "bk2", "bk3"):
+for _n in ("own", "lm", "heir", "heir2", "da", "db", "yha", "yhb", "bk0", "bk1", "bk2", "bk3"):
     SEMAPHORES.append("d_" + _n)
 for _k in range(8):
     _buf("b%d" % _k, 512, "float32", "psum")
@@ -134,12 +138,15 @@ def rank_program(g, core, T, topo):
     b = [T[k] for k in BANKS]
 
     load("y", T.lm0[:], T.lm[:], "d_lm", "lm0")
+    load("s", T.heirI[0:64, :], T.heir[:], "d_heir", "heirA")
+    load("s", T.heirI[64:128, :], T.heir[:], "d_heir2", "heirB")
     load("y", T.daI[:], T.da[:], "d_da", "daI")
-    for k in range(4):
-        load("s", T.W[:, 1024 * k:1024 * k + 1024], T.bk[:, 1024 * k:1024 * k + 1024], "d_bk%d" % k, "Wk%d" % k)
-    load("y", T.dbI[:], T.db[:], "d_db", "dbI")
+    load("s", T.dbI[:], T.db[:], "d_db", "dbI")
     load("y", T.ownI[:], T.own[:], "d_own", "ownI")
-    load("y", T.heirI[:], T.heir[:], "d_heir", "heirI")
+    PIECE = (0, 1536, 2560, 3584, 4096)
+    for k in range(4):
+        lo, hi = PIECE[k], PIECE[k + 1]
+        load("s" if k % 2 == 0 else "y", T.W[:, lo:hi], T.bk[:, lo:hi], "d_bk%d" % k, "Wk%d" % k)
     WK = ["Wk%d" % k for k in range(4)]
     HK = ["HN%d" % k for k in range(8)]
 
@@ -163,119 +170,165 @@ def rank_program(g, core, T, topo):
         send(T.cores[(rank + t) % n], T["lm%d" % t][:], T.lm0[:], "l%d" % t, "lm0")
         arrive("l%d" % t, "lm%d" % t, T.cores[(rank - t) % n])
 
-    def bits(out, in0, s1, op0, reads, writes, s2=None, op1=None):
-        ts(out, in0, s1, op0, reads, writes, s2, op1)
-
-    bits(T.p15i[:], T.pi[:], 15, A.bitwise_and, ["pi"], ["p15i"])
-    bits(T.p4i[:], T.pi[:], 4, A.arith_shift_right, ["pi"], ["p4i"])
-    bits(T.oddi[:], T.pi[:], 1, A.bitwise_and, ["pi"], ["oddi"])
+    BITS = (("pg", 3, 7), ("ph", 6, None), ("pk", 0, 7), ("p4", 4, None), ("p2", 1, 7), ("p15", 0, 15))
+    for k, sh, m in BITS:
+        ts(T[k + "i"][:], T.pi[:], sh, A.arith_shift_right, ["pi"], [k + "i"], m, A.bitwise_and if m else None)
     vcopy(T.pf[:], T.pi[:], ["pi"], ["pf"])
-    bits(T.c4i[:], T.ci[:], 4, A.arith_shift_right, ["ci"], ["c4i"])
-    bits(T.c15i[:], T.ci[:], 15, A.bitwise_and, ["ci"], ["c15i"])
-    bits(T.chi[:], T.ci[:], 1, A.arith_shift_right, ["ci"], ["chi"], 7, A.bitwise_and)
-    vcopy(T.p15[:], T.p15i[:], ["p15i"], ["p15"])
-    vcopy(T.p4[:], T.p4i[:], ["p4i"], ["p4"])
-    vcopy(T.odd[:], T.oddi[:], ["oddi"], ["odd"])
-    ts(T.E8[:], T.c4i[0:8, :], T.pf[0:8, :], A.is_equal, ["c4i", "pf"], ["E8"])
-    ts(T.ab[:, 0:256], T.daI[:, 0:256], BIAS, A.subtract, ["daI"], ["ab0"])
-    ts(T.C01[:], T.chi[:], 0, A.is_equal, ["chi"], ["C01"])
-    ts(T.C23[:], T.chi[:], 1, A.is_equal, ["chi"], ["C23"])
+    for k, sh, m in BITS:
+        vcopy(T[k][:], T[k + "i"][:], [k + "i"], [k])
+    ts(T.c4i[:], T.ci[:], 4, A.arith_shift_right, ["ci"], ["c4i"])
+    ts(T.th[:], T.pg[:], 16.0, A.mult, ["pg"], ["th"])
+    ts(T.pk[:], T.pk[:], 1.0, A.add, ["pk"], ["pk"])
+    ts(T.c15i[:], T.ci[:], 15, A.bitwise_and, ["ci"], ["c15i"])
+    tt(T.th[:], T.th[:], T.ph[:], A.add, ["th", "ph"], ["th"])
+    ts(T.tn[:], T.p4[:], 16.0, A.mult, ["p4"], ["tn"], 2.0, A.add)
+    ts(T.hb2[:], T.ph[:], -2048.0, A.mult, ["ph"], ["hb2"], 2048.0, A.add)
+    ts(T.Z2[:], T.ci[:], T.th[:], A.is_equal, ["ci", "th", "pk"], ["Z2"], T.pk[:], A.mult)
+    tt(T.tn[:], T.tn[:], T.p2[:], A.add, ["tn", "p2"], ["tn"])
     ts(T.BO[:], T.c4i[:], T.p4[:], A.is_equal, ["c4i", "p4"], ["BO"])
-    ts(T.maskP[:], T.c15i[:], T.p15[:], A.is_equal, ["c15i", "p15"], ["maskP"])
-    ts(T.nE8[:], T.E8[:], -1.0, A.mult, ["E8"], ["nE8"])
-    tt(T.E01[:], T.E8[:], T.C01[0:8, :], A.mult, ["E8", "C01"], ["E01"])
-    ts(T.bb[:, 0:256], T.dbI[:, 0:256], BIAS, A.subtract, ["dbI"], ["bb0"])
-    tt(T.WN[:], T.BO[:], T.C23[:], A.mult, ["BO", "C23"], ["WN"])
-    tt(T.B01[:], T.BO[:], T.C01[:], A.mult, ["BO", "C01"], ["B01"])
+    ts(T.E8[:], T.c4i[0:8, :], T.pf[0:8, :], A.is_equal, ["c4i", "pf"], ["E8"])
+    for k in range(8):
+        ts(T.WH[:, 128 * k:128 * k + 128], T.Z2[:], float(k + 1), A.is_equal, ["Z2"], ["WH%d" % k])
+    ts(T.hcut[0:64, :], T.heirI[0:64, :], 4080, A.bitwise_and, ["heirA"], ["hcA"])
+    ts(T.hcut[64:128, :], T.heirI[64:128, :], 15, A.bitwise_and, ["heirB"], ["hcB"])
+    ts(T.C01[:], T.c15i[:], 1, A.is_le, ["c15i"], ["C01"])
+    ts(T.Hs[:], T.hcut[:], T.hb2[:], A.subtract, ["hcA", "hcB", "hb2"], ["Hs"])
     ts(T.l01[:], T.p15[:], 1.0, A.is_le, ["p15"], ["l01"])
-    ts(T.l03[:], T.p15[:], 3.0, A.is_le, ["p15"], ["l03"])
-    ts(T.p16[:], T.p15[:], 1.0, A.add, ["p15"], ["p16"])
-    tt(T.l23[:], T.l03[:], T.l01[:], A.subtract, ["l03", "l01"], ["l23"])
-    tt(T.m13[:], T.l03[:], T.odd[:], A.mult, ["l03", "odd"], ["m13"])
-    ts(T.Z2[:], T.B01[:], T.p16[:], A.mult, ["B01", "p16"], ["Z2"], 1.0, A.subtract)
+    ts(T.l29[:], T.p15[:], 9.0, A.is_le, ["p15"], ["l29"])
+    ts(T.WN[:], T.ci[:], T.tn[:], A.is_equal, ["ci", "tn"], ["WN"])
+    ts(T.nE8[:], T.E8[:], -1.0, A.mult, ["E8"], ["nE8"])
+    tt(T.l29[:], T.l29[:], T.l01[:], A.subtract, ["l29", "l01"], ["l29"])
+    tt(T.E01[:], T.E8[:], T.C01[0:8, :], A.mult, ["E8", "C01"], ["E01"])
+    ts(T.m1[:], T.p15[:], 1.0, A.is_equal, ["p15"], ["m1"])
+    ts(T.cb[:], T.l29[:], -256.0, A.mult, ["l29"], ["cb"])
+    ts(T.ncb[:], T.l29[:], 256.0, A.mult, ["l29"], ["ncb"])
+    ts(T.maskP[:], T.c15i[:], T.p15[:], A.is_equal, ["c15i", "p15"], ["maskP"])
+
+    XB = (2, 3, 0, 1, 7, 2, 3, 0)
+
+    def x_heir(k):
+        bk = "b%d" % XB[k]
+        mm(T[bk][:], T.WH[:, 128 * k:128 * k + 128], T.Hs[:], True, False, ["WH%d" % k, "Hs"], [bk])
+
+    def x_book(k):
+        bk = "b%d" % XB[k]
+        wk = "Wk%d" % (0 if k < 3 else 1 if k < 5 else 2 if k < 7 else 3)
+        mm(T[bk][:], T.WN[:], T.W[:, 512 * k:512 * k + 512], False, True, ["WN", wk], [bk])
+
+    def x_copy(k):
+        bk = "b%d" % XB[k]
+        if k in VCOPY:
+            ts(T.HN[:, 512 * k:512 * k + 512], T[bk][:], T.cb[:], A.add, [bk, "cb"], ["HN%d" % k])
+        else:
+            act(T.HN[:, 512 * k:512 * k + 512], T[bk][:], [bk, "cb"], ["HN%d" % k], func=F.Identity, bias=T.cb[:])
+
+    CUT = (0, 256, 512, 1280)
+
+    def indices(k, what="ab"):
+        lo, hi = CUT[k], CUT[k + 1]
+        if "a" in what:
+            ts(T.ab[:, lo:hi], T.daI[:, lo:hi], BIAS, A.subtract, ["daI"], ["ab%d" % k])
+        if "b" in what:
+            ts(T.bb[:, lo:hi], T.dbI[:, lo:hi], BIAS, A.subtract, ["dbI"], ["bb%d" % k])
+
+    indices(0)
     ts(T.ownH[:], T.ownI[:], BIAS, A.subtract, ["ownI"], ["ownH"])
 
-    AR = [(0, 256), (256, 768), (768, 1280)]
+    AK = {0: 1, 1: 2, 3: 3}
+    AR = [(0, 256), (256, 512), (512, 1024), (1024, 1280)]
 
     def rng(t):
-        return 0 if t == 0 else 1 if t < 3 else 2
+        return (0, 1, 2, 2, 3)[t]
 
-    def build_an(k):
+    def an_t(k):
         lo, hi = AR[k]
         w = hi - lo
-        kk = "0" if k == 0 else "1"
-        mm(b[0][:, 0:w], T.E8[:], T.ab[:, lo:hi], True, True, ["E8", "ab" + kk], ["b0"])
-        act(T.AN[:, lo:hi], b[0][:, 0:w], ["b0"], ["AN%d" % k])
-        mm(b[1][:, 0:w], T.E8[:], T.bb[:, lo:hi], True, False, ["E8", "bb" + kk], ["b1"])
-        mm(b[1][:, 0:w], T.nE8[:], T.ab[:, lo:hi], False, True, ["nE8", "ab" + kk], ["b1"])
-        act(T.BA[:, lo:hi], b[1][:, 0:w], ["b1"], ["BA%d" % k])
+        kk = str(min(k, 2))
+        mm(b[5][:, 0:w], T.E8[:], T.ab[:, lo:hi], True, True, ["E8", "ab" + kk], ["b5"])
+        mm(b[6][:, 0:w], T.E8[:], T.bb[:, lo:hi], True, False, ["E8", "bb" + kk], ["b6"])
+        mm(b[6][:, 0:w], T.nE8[:], T.ab[:, lo:hi], False, True, ["nE8", "ab" + kk], ["b6"])
 
-    build_an(0)
+    def an_s(k):
+        lo, hi = AR[k]
+        act(T.AN[:, lo:hi], b[5][:, 0:hi - lo], ["b5"], ["AN%d" % k])
+        act(T.BA[:, lo:hi], b[6][:, 0:hi - lo], ["b6"], ["BA%d" % k])
+
+    def prep_bank(t):
+        return "b4" if t == 0 else "b7"
 
     def prep_t(t):
-        kk = "0" if t == 0 else "1"
+        kk = str(min(t, 2))
         lk = "lm%d" % (t % n)
-        mm(b[7][:, 0:256], T.WN[:], T[lk][:], True, False, ["WN", lk], ["b7"])
-        mm(b[7][:, 0:256], T.E01[:], T.bb[:, 256 * t:256 * t + 256], False, True, ["E01", "bb" + kk], ["b7"])
+        bk = prep_bank(t)
+        mm(T[bk][:, 0:256], T.WN[:], T[lk][:], True, False, ["WN", lk], [bk])
+        mm(T[bk][:, 0:256], T.E01[:], T.bb[:, 256 * t:256 * t + 256], False, True, ["E01", "bb" + kk], [bk])
         for ch in range(2):
-            mm(b[7][:, 256 + 128 * ch:384 + 128 * ch], T.ab[:, 256 * t + 128 * ch:256 * t + 128 * ch + 128], T.E8[:], True, True,
-               ["ab" + kk, "E8"], ["b7"])
+            mm(T[bk][:, 256 + 128 * ch:384 + 128 * ch], T.ab[:, 256 * t + 128 * ch:256 * t + 128 * ch + 128], T.E8[:], True, True,
+               ["ab" + kk, "E8"], [bk])
 
     def prep_s(t):
-        act(T.Yn[:], b[7][:, 0:256], ["b7", "m13"], ["Yn"], scale=T.m13[:])
+        bk = prep_bank(t)
+        act(T.Yn[:], T[bk][:, 0:256], [bk, "m1", "ncb"], ["Yn"], func=F.Identity, scale=T.m1[:], bias=T.ncb[:])
 
     def prep_nh(t):
-        tt(T["NH%d" % (t % 2)][:], b[7][:, 0:256], T.Yn[:], A.subtract, ["b7", "Yn"], ["NH%d" % (t % 2)])
+        bk = prep_bank(t)
+        tt(T["NH%d" % (t % 2)][:], T[bk][:, 0:256], T.Yn[:], A.subtract, [bk, "Yn"], ["NH%d" % (t % 2)])
 
     def prep_ma(t):
-        k = "MA%d" % (t % 2)
+        k, bk = "MA%d" % (t % 2), prep_bank(t)
         for ch in range(2):
-            tt(T[k][:, 128 * ch:128 * ch + 128], b[7][:, 256 + 128 * ch:384 + 128 * ch], T.maskP[:], A.mult, ["b7", "maskP"], [k + "c%d" % ch])
+            tt(T[k][:, 128 * ch:128 * ch + 128], T[bk][:, 256 + 128 * ch:384 + 128 * ch], T.maskP[:], A.mult, [bk, "maskP"], [k + "c%d" % ch])
 
-    def rep(t, q, who):
+    def rep(t, qs, who):
         k = "lm%d" % t
-        if who == "v":
-            vcopy(T["lr%d" % t][:, q:4096:16], T[k][:], [k], ["lr%d_%d" % (t, q)])
-        else:
-            act(T["lr%d" % t][:, q:4096:16], T[k][:], [k], ["lr%d_%d" % (t, q)])
+        for q in qs:
+            if who == "v":
+                vcopy(T["lr%d" % t][:, q:4096:16], T[k][:], [k], ["lr%d_%d" % (t, q)])
+            else:
+                act(T["lr%d" % t][:, q:4096:16], T[k][:], [k], ["lr%d_%d" % (t, q)])
 
-    prep_t(0)
-    prep_s(0)
-    ts(T.K1[:], T.BO[:, 0:128:16], 1.0, A.mult, ["BO"], ["K1"])
-    ts(T.K4[:], T.BO[:, 0:128:16], 4096.0, A.mult, ["BO"], ["K4"])
-    prep_ma(0)
-    prep_nh(0)
-    for q in range(10):
-        rep(0, q, "s")
+    def own_of(t, ch):
+        if t == 0:
+            return T.ownH[:, 128 * ch:128 * ch + 128], "ownH"
+        return b[2 + ch][:, 0:128], "b%d" % (2 + ch)
 
-    def deeds(t, ch):
+    def deeds_hit(t, ch):
         c = str(ch)
         k = str(rng(t))
         cols = slice(256 * t + 128 * ch, 256 * t + 128 * ch + 128)
-        loc = slice(128 * ch, 128 * ch + 128)
-        if t == 0:
-            own, ok = T.ownH[:, loc], "ownH"
-        else:
+        if t:
             rk = "R%d%d" % (t, ch)
             mm(b[2 + ch][:, 0:128], T[rk][:], T.IdH[:], True, True, [rk, "IdH"], ["b%d" % (2 + ch)])
-            own, ok = b[2 + ch][:, 0:128], "b%d" % (2 + ch)
+        own, ok = own_of(t, ch)
         tt(T["HT" + c][:], own, T.AN[:, cols], A.is_equal, [ok, "AN" + k], ["HT" + c])
         mm(b[5 + ch][:, 0:128], T["HT" + c][:], T.BO[:], True, True, ["HT" + c, "BO"], ["b%d" % (5 + ch)])
         tt(T["hb" + c][:], T["HT" + c][:], T.BA[:, cols], A.mult, ["HT" + c, "BA" + k], ["hb" + c])
+
+    def deeds_list(t, ch):
+        c = str(ch)
+        loc = slice(128 * ch, 128 * ch + 128)
+        own, ok = own_of(t, ch)
         tt(T["X" + c][:], b[5 + ch][:, 0:128], T.maskP[:], A.min, ["b%d" % (5 + ch), "maskP"], ["X" + c])
         m = "MA%d" % (t % 2)
         lst = b[4][:, 8 * ch:8 * ch + 8]
         mm(lst, T[m][:, loc], T.K1[:], True, False, [m + "c" + c, "K1"], ["b4"])
         mm(lst, T["X" + c][:], T.K4[:], False, True, ["X" + c, "K4"], ["b4"])
         tt(T["ownN" + c][:], own, T["hb" + c][:], A.add, [ok, "hb" + c], ["ownN" + c])
-        ts(T["LS" + c][:], lst, BIAS, A.add, ["b4"], ["LS" + c])
 
-    def scatters(t, ch):
+    def deeds_end(ch):
+        c = str(ch)
+        ts(T["LS" + c][:], b[4][:, 8 * ch:8 * ch + 8], BIAS, A.add, ["b4"], ["LS" + c])
+
+    def scatter_h(t, ch):
         c = str(ch)
         h = "NH%d" % (t % 2)
-        l = "lm%d" % (t % n)
         loc = slice(128 * ch, 128 * ch + 128)
         vcopy(T.HN[:, 0:8192].indirect(T["LS" + c][:, 0:8]), T[h][:, loc], ["LS" + c, h], HK)
+
+    def scatter_w(t, ch):
+        c = str(ch)
+        l = "lm%d" % (t % n)
+        loc = slice(128 * ch, 128 * ch + 128)
         vcopy(T.W[:, 0:8192].indirect(T["LS" + c][:, 0:8]), T[l][:, loc], ["LS" + c, l], WK)
 
     def offs(ch):
@@ -292,15 +345,12 @@ def rank_program(g, core, T, topo):
         a, z = 128 * ch + lo, 128 * ch + hi
         act(T["H%d" % ch][:, 16 * lo:16 * hi], T.HN[:, 0:4096].indirect(T.off[:, a:z]), HK + ["off%d" % ch], ["H%d_%d" % (ch, lo)])
 
-    VS, SS = 96, 64
     MK = {c: ["M%d_0" % c, "M%d_%d" % (c, VS)] for c in (0, 1)}
     HHK = {c: ["H%d_0" % c, "H%d_%d" % (c, SS)] for c in (0, 1)}
 
-    def gv_whole(t, ch):
+    def gather_whole(t, ch):
         gv(t, ch, 0, 128)
         wr[MK[ch][1]] = dict(wr[MK[ch][0]])
-
-    def gs_whole(ch):
         gs(ch, 0, 128)
         wr[HHK[ch][1]] = dict(wr[HHK[ch][0]])
 
@@ -313,11 +363,9 @@ def rank_program(g, core, T, topo):
             for k in (1, 2):
                 mm(b[ch][:, 128 * k:128 * k + 128], T.HI2[:, 0:128], T["OT%d" % ch][:], False, False, ["HI2", "OT%d" % ch], [bk])
 
-    def hmm(ch):
+    def sums(ch):
         for q in range(16):
             mm(b[ch][:, q:384:16], T["H%d" % ch][:, q:2048:16], T.RH[:], False, False, HHK[ch] + ["RH"], ["b%d" % ch])
-
-    def mmm(ch):
         for q in range(16):
             mm(b[ch][:, q:128:16], T["M%d" % ch][:, q:2048:16], T.RM[:], False, q == 15, MK[ch] + ["RM"], ["b%d" % ch])
 
@@ -335,40 +383,53 @@ def rank_program(g, core, T, topo):
     def conv(ch):
         ts(T.off[:, 128 * ch:128 * ch + 128], b[2 + ch][:, 0:128], BIAS, A.add, ["b%d" % (2 + ch)], ["off%d" % ch])
 
-    deeds(0, 0)
-    deeds(0, 1)
-    ts(T.Hs[:], T.heirI[:], BIAS, A.subtract, ["heirI"], ["Hs"])
-    for k in range(16):
-        ts(T.WH[:, 128 * k:128 * k + 128], T.Z2[:], float(k), A.is_equal, ["Z2"], ["WH%d" % k])
-    offs(0)
-    offs(1)
-    ts(T.nBO[:], T.BO[:], -1.0, A.mult, ["BO"], ["nBO"])
+    act(T.nBO[:], T.BO[:], ["BO"], ["nBO"], scale=-1.0)
+    act(T.RM[:], T.BO[:, 0:128:16], ["BO"], ["RM"], scale=2.0)
+    act(T.K4[:], T.BO[:, 0:128:16], ["BO"], ["K4"], scale=4096.0)
+    for k in (0, 1):
+        x_heir(k)
+    an_t(0)
+    an_s(0)
+    prep_t(0)
+    prep_s(0)
+    for k in (2, 3, 4):
+        x_heir(k)
+    ts(T.K1[:], T.BO[:, 0:128:16], 1.0, A.mult, ["BO"], ["K1"])
+    indices(1)
+    prep_ma(0)
+    prep_nh(0)
+    for k in (0, 1, 2):
+        x_book(k)
+    rep(0, range(6), "s")
+    x_copy(0)
+    deeds_hit(0, 0)
+    deeds_hit(0, 1)
+    x_heir(5)
+    x_copy(1)
+    x_copy(2)
     ts(T.HI2[:, 0:128], T.ci[:], T.pf[:], A.is_equal, ["ci", "pf"], ["HI2"], 0.5, A.mult)
     ts(T.HI2[:, 128:256], T.ci[:], T.pf[:], A.is_equal, ["ci", "pf"], ["HI2"], 0.5, A.mult)
-    ts(T.RM[:], T.BO[:, 0:128:16], 2.0, A.mult, ["BO"], ["RM"])
-    ts(T.RH[:, 0:8], T.BO[:, 0:128:16], T.l23[:], A.mult, ["BO", "l23"], ["RH"], -1.0, A.mult)
+    deeds_list(0, 0)
+    deeds_list(0, 1)
+    x_heir(6)
+    x_heir(7)
+    rep(0, range(6, 16 - VR0), "s")
+    ts(T.RH[:, 0:8], T.BO[:, 0:128:16], T.l29[:], A.mult, ["BO", "l29"], ["RH"], -1.0, A.mult)
     ts(T.RH[:, 8:16], T.BO[:, 0:128:16], T.l01[:], A.mult, ["BO", "l01"], ["RH"], -0.5, A.mult)
     ts(T.RH[:, 16:24], T.BO[:, 0:128:16], T.l01[:], A.mult, ["BO", "l01"], ["RH"], 0.5, A.mult)
-    for q in range(10, 16):
-        rep(0, q, "v")
     ts(T.IdH[:], T.ci[:], T.pf[:], A.is_equal, ["ci", "pf"], ["IdH"])
-    ts(T.ab[:, 256:1280], T.daI[:, 256:1280], BIAS, A.subtract, ["daI"], ["ab1"])
-    ts(T.bb[:, 256:1280], T.dbI[:, 256:1280], BIAS, A.subtract, ["dbI"], ["bb1"])
-    build_an(1)
-    build_an(2)
-    XB = (0, 1, 7)
-    for k in range(8):
-        x = XB[k % 3]
-        bk = "b%d" % x
-        y = "Yx%d" % (k % 2)
-        mm(b[x][:], T.WN[:], T.W[:, 512 * k:512 * k + 512], True, False, ["WN", "Wk%d" % (k // 2)], [bk])
-        for j in range(2):
-            w = 2 * k + j
-            mm(b[x][:, 256 * j:256 * j + 256], T.WH[:, 128 * w:128 * w + 128], T.Hs[:], False, j == 1, ["WH%d" % w, "Hs"], [bk])
-        act(T[y][:], b[x][:], [bk, "m13"], [y], scale=T.m13[:])
-        tt(T.HN[:, 512 * k:512 * k + 512], b[x][:], T[y][:], A.subtract, [bk, y], ["HN%d" % k])
-    scatters(0, 0)
-    scatters(0, 1)
+    offs(0)
+    offs(1)
+    deeds_end(0)
+    deeds_end(1)
+    for k in range(3, 8):
+        x_book(k)
+        x_copy(k)
+    rep(0, range(16 - VR0, 16), "v")
+    scatter_w(0, 0)
+    scatter_h(0, 0)
+    scatter_h(0, 1)
+    scatter_w(0, 1)
 
     nxt = T.cores[(rank + 1) % n]
     prv = T.cores[(rank - 1) % n]
@@ -376,29 +437,36 @@ def rank_program(g, core, T, topo):
         for ch in range(2):
             arrive("r%d%d" % (t, ch), "R%d%d" % (t, ch), prv)
 
-    def yh_part(ks):
-        for k in ks:
-            mm(b[4][:, 0:256], T.WY[:, 128 * k:128 * k + 128], T.HN[:, 256 * k:256 * k + 256], k == 0, k == 15,
-               ["WY%d" % k] + HK, ["b4"])
+    def out_yo(ch):
+        loc = slice(128 * ch, 128 * ch + 128)
+        ts(T.yof[:, loc], b[2 + ch][:, 0:128], float(BIAS), A.add, ["b%d" % (2 + ch)], ["yof%d" % ch])
+        op("y", lambda: g.sync.dma_start(out=T.yo[:, loc], in_=T.yof[:, loc]), ["yof%d" % ch], [], "dout", 16)
 
     for t in range(R):
         last = t == R - 1
         if t:
-            deeds(t, 0)
-            offs(0)
-            scatters(t, 0)
-            deeds(t, 1)
-            scatters(t, 1)
-            offs(1)
+            for ch in (0, 1):
+                deeds_hit(t, ch)
+                deeds_list(t, ch)
+                if ch == 0:
+                    offs(0)
+                deeds_end(ch)
+                scatter_h(t, ch)
+                scatter_w(t, ch)
         init(t, 0, 0)
         init(t, 1, 0)
-        gv_whole(t, 0)
-        gs_whole(0)
+        if not last:
+            prep_t(t + 1)
+        if t in AK:
+            an_t(AK[t])
+        gather_whole(t, 0)
+        if t:
+            offs(1)
         if last:
+            for k, lane in (("yha", 0), ("yhb", 1)):
+                op("y", lambda: g.sync.dma_start(out=T[k][:], in_=T.HN[lane:128:16, 0:4096]), HK, [k], "d_" + k, 16)
             op("y", lambda: g.sync.dma_start(out=T.yd[:], in_=T.W[:, 0:4096]), WK, [], "dout", 16)
-            yh_part(range(0, 8))
-        hmm(0)
-        mmm(0)
+        sums(0)
         gv(t, 1, 0, VS)
         gs(1, 0, SS)
         sign(0)
@@ -406,69 +474,47 @@ def rank_program(g, core, T, topo):
         upd(0, "OT0")
         turn(0, "OT0")
         init(t, 0, 1)
-        if last:
-            yh_part(range(8, 12))
-        else:
-            prep_t(t + 1)
         gv(t, 1, VS, 128)
         conv(0)
-        hmm(1)
-        mmm(1)
+        sums(1)
         gv(t, 0, 0, VS)
         gs(0, 0, SS)
         sign(1)
         gs(0, SS, 128)
+        if last:
+            act(T.yh2[:], T.yha[:], ["yha"], ["yh2"], bias=float(BIAS))
         upd(1, "OT1")
         turn(1, "OT1")
-        init(t, 1, 1)
-        if last:
-            yh_part(range(12, 16))
-        gv(t, 0, VS, 128)
         conv(1)
-        hmm(0)
-        mmm(0)
-        gv(t, 1, 0, VS)
-        gs(1, 0, SS)
+        init(t, 1, 1)
+        gv(t, 0, VS, 128)
+        sums(0)
+        gather_whole(t, 1)
         sign(0)
-        gs(1, SS, 128)
+        sums(1)
         if not last:
             upd(0, "SD%d0" % t)
             send(nxt, T["R%d0" % (t + 1)][:], T["SD%d0" % t][:], "r%d0" % (t + 1), "SD%d0" % t)
-            gv(t, 1, VS, 128)
             prep_s(t + 1)
-            hmm(1)
-            mmm(1)
+            if t in AK:
+                an_s(AK[t])
             prep_ma(t + 1)
-            if t + 1 < n:
-                for q in range(12, 16):
-                    rep(t + 1, q, "v")
+            if t == 0:
+                indices(2, "a")
             sign(1)
             upd(1, "SD%d1" % t)
             send(nxt, T["R%d1" % (t + 1)][:], T["SD%d1" % t][:], "r%d1" % (t + 1), "SD%d1" % t)
             prep_nh(t + 1)
             if t + 1 < n:
-                for q in range(12):
-                    rep(t + 1, q, "s")
-            if t == R - 2:
-                vcopy(T.C16[:], T.c15i[:], ["c15i"], ["C16"])
-                ts(T.C16[:], T.C16[:], 1.0, A.add, ["C16"], ["C16"])
-                tt(T.C16[:], T.C16[:], T.BO[:], A.mult, ["C16", "BO"], ["C16"])
-                ts(T.Z3[:], T.C16[:], T.l01[:], A.mult, ["C16", "l01"], ["Z3"], 1.0, A.subtract)
-                for k in range(16):
-                    ts(T.WY[:, 128 * k:128 * k + 128], T.Z3[:], float(k), A.is_equal, ["Z3"], ["WY%d" % k])
+                rep(t + 1, range(16 - VR, 16), "v")
+                rep(t + 1, range(16 - VR), "s")
+            if t == 0:
+                indices(2, "b")
         else:
+            tt(T.yhf[:], T.yh2[:], T.yhb[:], A.add, ["yh2", "yhb"], ["yhf"])
+            op("y", lambda: g.sync.dma_start(out=T.yh[:], in_=T.yhf[:]), ["yhf"], [], "dout", 16)
             upd(0, "OT0")
             turn(0, "OT0")
-            gv(t, 1, VS, 128)
-
-            def out_yo(ch):
-                loc = slice(128 * ch, 128 * ch + 128)
-                ts(T.yof[:, loc], b[2 + ch][:, 0:128], float(BIAS), A.add, ["b%d" % (2 + ch)], ["yof%d" % ch])
-                op("y", lambda: g.sync.dma_start(out=T.yo[:, loc], in_=T.yof[:, loc]), ["yof%d" % ch], [], "dout", 16)
-            hmm(1)
-            mmm(1)
-            ts(T.yhf[:], b[4][:, 0:256], float(BIAS), A.add, ["b4"], ["yhf"])
-            op("y", lambda: g.sync.dma_start(out=T.yh[:], in_=T.yhf[:]), ["yhf"], [], "dout", 16)
             out_yo(0)
             sign(1)
             upd(1, "OT1")

@@ -2,10 +2,12 @@ from concourse.mybir import AluOpType as A, ActivationFunctionType as F
 
 BIAS = 2048
 TH = 136.5 + 2048
+BIG = 8192
+KS = 256.0
 R = 5
-VS, SS = 104, 88
-VR0, VR = 2, 3
-VCOPY = (1, 4, 6)
+VA, VB, VC, SA, SB = 112, 112, 112, 104, 104
+S0, VR, RB = 10, 2, 3
+N0 = 5
 
 SCRATCH = {}
 SEMAPHORES = ["v", "s", "t", "p", "loc", "dout"]
@@ -15,29 +17,30 @@ def _buf(name, cols, dtype, where="sbuf", rows=128):
     SCRATCH[name] = (where, [rows, cols], dtype)
 
 
-for _n, _c in (("pi", 1), ("ci", 128), ("p15i", 1), ("p4i", 1), ("p2i", 1), ("pki", 1), ("pgi", 1), ("phi", 1),
-               ("c15i", 128), ("c4i", 128), ("ownI", 256), ("heirI", 512), ("hcut", 512)):
-    _buf(_n, _c, "int32")
-_buf("daI", 1280, "int32", rows=8)
-_buf("dbI", 1280, "int32", rows=8)
-for _n in ("pf", "p15", "p4", "p2", "pk", "pg", "ph", "tn", "th", "hb2", "l01", "l29", "m1", "cb", "ncb"):
-    _buf(_n, 1, "float32")
-for _n, _c in (("BO", 128), ("nBO", 128), ("maskP", 128), ("C01", 128), ("WN", 128), ("Z2", 128),
-               ("RM", 8), ("RH", 24), ("K4", 8), ("yha", 256), ("yhb", 256),
-               ("W", 8192), ("HN", 8192), ("M0", 2048), ("M1", 2048), ("H0", 2048), ("H1", 2048),
-               ("Yn", 256), ("NH0", 256), ("NH1", 256), ("HT0", 128), ("HT1", 128), ("X0", 128), ("X1", 128),
-               ("SG0", 128), ("SG1", 128), ("lm0", 256), ("lm1", 256), ("lm2", 256), ("lm3", 256),
+_buf("D0", 128, "int32")
+_buf("V8", 8, "int32")
+_buf("NS", 512, "float32", rows=64)
+_buf("Hf", 512, "float32", rows=64)
+_buf("ownI", 256, "int32")
+for _n, _c, _r in (("e8i", 128, 16), ("e0i", 128, 16), ("e16i", 128, 16), ("heirI", 512, 64), ("dI", 1280, 16)):
+    _buf(_n, _c, "int32", rows=_r)
+for _n, _c in (("cb", 1), ("NH0", 256), ("NH1", 256), ("AN", 1280), ("hb0", 128), ("hb1", 128),
+               ("tt0", 128), ("tt1", 128), ("yof", 256), ("HN", 8192)):
+    _buf(_n, _c, "float32")
+for _n, _c in (("BO", 128), ("nBO", 128), ("maskP", 128), ("RM", 8), ("K4", 8), ("BI", 128), ("WN", 128), ("WNK", 512),
+               ("W", 8192), ("M00", 2048), ("M01", 2048), ("M10", 2048), ("M11", 2048),
+               ("HT0", 128), ("HT1", 128), ("X0", 128), ("X1", 128), ("n0", 128), ("n1", 128), ("m0", 128), ("m1", 128),
+               ("lm0", 256), ("lm1", 256), ("lm2", 256), ("lm3", 256),
                ("lr0", 4096), ("lr1", 4096), ("lr2", 4096), ("lr3", 4096)):
     _buf(_n, _c, "bfloat16")
-for _n, _c in (("IdH", 128), ("HI2", 256), ("WH", 1024), ("K1", 8), ("Hs", 512), ("ownH", 256), ("ownN0", 128), ("ownN1", 128),
-               ("OT0", 128), ("OT1", 128), ("MA0", 256), ("MA1", 256)):
+for _n, _c in (("EA", 128), ("EP", 128), ("EN", 128), ("EB", 128), ("E0", 128), ("E16", 128), ("ib", 1280)):
+    _buf(_n, _c, "float16", rows=16)
+for _n, _c in (("IdH", 128), ("nIdH", 256), ("RH", 24), ("K1", 8), ("ownH", 256), ("MA0", 256), ("MA1", 256),
+               ("ownN0", 128), ("ownN1", 128), ("Hc0", 128), ("Hc1", 128), ("XX0", 128), ("XX1", 128),
+               ("OT0", 128), ("OT1", 128), ("H00", 2048), ("H01", 2048), ("H10", 2048), ("H11", 2048)):
     _buf(_n, _c, "float16")
-for _n, _c in (("E8", 128), ("nE8", 128), ("E01", 128), ("ab", 1280), ("bb", 1280)):
-    _buf(_n, _c, "float16", rows=8)
-for _n, _c in (("AN", 1280), ("BA", 1280), ("hb0", 128), ("hb1", 128), ("tt0", 128), ("tt1", 128),
-               ("yof", 256), ("yh2", 256), ("yhf", 256)):
-    _buf(_n, _c, "float32")
-_buf("off", 256, "uint16")
+_buf("off0", 256, "uint16")
+_buf("off1", 256, "uint16")
 _buf("LS0", 8, "uint16")
 _buf("LS1", 8, "uint16")
 for _t in range(4):
@@ -47,7 +50,7 @@ for _t in range(4):
         SEMAPHORES.append("r%d%d" % (_t + 1, _c))
 for _t in (1, 2, 3):
     SEMAPHORES.append("l%d" % _t)
-for _n in ("own", "lm", "heir", "heir2", "da", "db", "yha", "yhb", "bk0", "bk1", "bk2", "bk3"):
+for _n in ("own", "lm", "heir", "da", "db", "bk0", "bk1", "bk2", "bk3", "hr", "nr"):
     SEMAPHORES.append("d_" + _n)
 for _k in range(8):
     _buf("b%d" % _k, 512, "float32", "psum")
@@ -132,26 +135,33 @@ def rank_program(g, core, T, topo):
     def mm(out, lhsT, rhs, start, stop, reads, writes):
         op("t", lambda: g.tensor.matmul(out=out, lhsT=lhsT, rhs=rhs, start=start, stop=stop), reads, writes)
 
+    def iota(name, pattern, base, cm):
+        op("p", lambda: g.iota(T[name][:], pattern, base, cm), [], [name])
+
     def load(q, out, in_, sem, key):
         op(q, lambda: eng[q].dma_start(out=out, in_=in_), [], [key], sem, 16)
 
     b = [T[k] for k in BANKS]
 
+    load("s", T.heirI[:], T.heir[:], "d_heir", "heirI")
+    load("y", T.dI[0:8, :], T.da[:], "d_da", "daI")
+    load("s", T.dI[8:16, :], T.db[:], "d_db", "dbI")
     load("y", T.lm0[:], T.lm[:], "d_lm", "lm0")
-    load("s", T.heirI[0:64, :], T.heir[:], "d_heir", "heirA")
-    load("s", T.heirI[64:128, :], T.heir[:], "d_heir2", "heirB")
-    load("y", T.daI[:], T.da[:], "d_da", "daI")
-    load("s", T.dbI[:], T.db[:], "d_db", "dbI")
     load("y", T.ownI[:], T.own[:], "d_own", "ownI")
     PIECE = (0, 1536, 2560, 3584, 4096)
     for k in range(4):
         lo, hi = PIECE[k], PIECE[k + 1]
         load("s" if k % 2 == 0 else "y", T.W[:, lo:hi], T.bk[:, lo:hi], "d_bk%d" % k, "Wk%d" % k)
     WK = ["Wk%d" % k for k in range(4)]
-    HK = ["HN%d" % k for k in range(8)]
+    FK = ["HN%d" % k for k in range(8)]
+    HK = FK + ["HNh", "HNn"]
 
-    op("p", lambda: g.iota(T.pi[:], [[0, 1]], 0, 1), [], ["pi"])
-    op("p", lambda: g.iota(T.ci[:], [[1, 128]], 0, 0), [], ["ci"])
+    iota("e8i", [[1, 8], [0, 16]], 0, -1)
+    iota("e16i", [[0, 8], [1, 16]], 0, -1)
+    iota("e0i", [[1, 128]], 128, -16)
+    iota("D0", [[1, 128]], 0, -1)
+    iota("V8", [[16, 8]], 0, -1)
+    op("p", lambda: g.iota(T.HN[:, 2560:4096], [[0, 1536]], 0, 0, allow_small_or_imprecise_dtypes=True), [], FK[5:])
 
     def send(dst, out, in_, sem, key):
         wait("p", deps_of("p", [key], []))
@@ -170,114 +180,41 @@ def rank_program(g, core, T, topo):
         send(T.cores[(rank + t) % n], T["lm%d" % t][:], T.lm0[:], "l%d" % t, "lm0")
         arrive("l%d" % t, "lm%d" % t, T.cores[(rank - t) % n])
 
-    BITS = (("pg", 3, 7), ("ph", 6, None), ("pk", 0, 7), ("p4", 4, None), ("p2", 1, 7), ("p15", 0, 15))
-    for k, sh, m in BITS:
-        ts(T[k + "i"][:], T.pi[:], sh, A.arith_shift_right, ["pi"], [k + "i"], m, A.bitwise_and if m else None)
-    vcopy(T.pf[:], T.pi[:], ["pi"], ["pf"])
-    for k, sh, m in BITS:
-        vcopy(T[k][:], T[k + "i"][:], [k + "i"], [k])
-    ts(T.c4i[:], T.ci[:], 4, A.arith_shift_right, ["ci"], ["c4i"])
-    ts(T.th[:], T.pg[:], 16.0, A.mult, ["pg"], ["th"])
-    ts(T.pk[:], T.pk[:], 1.0, A.add, ["pk"], ["pk"])
-    ts(T.c15i[:], T.ci[:], 15, A.bitwise_and, ["ci"], ["c15i"])
-    tt(T.th[:], T.th[:], T.ph[:], A.add, ["th", "ph"], ["th"])
-    ts(T.tn[:], T.p4[:], 16.0, A.mult, ["p4"], ["tn"], 2.0, A.add)
-    ts(T.hb2[:], T.ph[:], -2048.0, A.mult, ["ph"], ["hb2"], 2048.0, A.add)
-    ts(T.Z2[:], T.ci[:], T.th[:], A.is_equal, ["ci", "th", "pk"], ["Z2"], T.pk[:], A.mult)
-    tt(T.tn[:], T.tn[:], T.p2[:], A.add, ["tn", "p2"], ["tn"])
-    ts(T.BO[:], T.c4i[:], T.p4[:], A.is_equal, ["c4i", "p4"], ["BO"])
-    ts(T.E8[:], T.c4i[0:8, :], T.pf[0:8, :], A.is_equal, ["c4i", "pf"], ["E8"])
-    for k in range(8):
-        ts(T.WH[:, 128 * k:128 * k + 128], T.Z2[:], float(k + 1), A.is_equal, ["Z2"], ["WH%d" % k])
-    ts(T.hcut[0:64, :], T.heirI[0:64, :], 4080, A.bitwise_and, ["heirA"], ["hcA"])
-    ts(T.hcut[64:128, :], T.heirI[64:128, :], 15, A.bitwise_and, ["heirB"], ["hcB"])
-    ts(T.C01[:], T.c15i[:], 1, A.is_le, ["c15i"], ["C01"])
-    ts(T.Hs[:], T.hcut[:], T.hb2[:], A.subtract, ["hcA", "hcB", "hb2"], ["Hs"])
-    ts(T.l01[:], T.p15[:], 1.0, A.is_le, ["p15"], ["l01"])
-    ts(T.l29[:], T.p15[:], 9.0, A.is_le, ["p15"], ["l29"])
-    ts(T.WN[:], T.ci[:], T.tn[:], A.is_equal, ["ci", "tn"], ["WN"])
-    ts(T.nE8[:], T.E8[:], -1.0, A.mult, ["E8"], ["nE8"])
-    tt(T.l29[:], T.l29[:], T.l01[:], A.subtract, ["l29", "l01"], ["l29"])
-    tt(T.E01[:], T.E8[:], T.C01[0:8, :], A.mult, ["E8", "C01"], ["E01"])
-    ts(T.m1[:], T.p15[:], 1.0, A.is_equal, ["p15"], ["m1"])
-    ts(T.cb[:], T.l29[:], -256.0, A.mult, ["l29"], ["cb"])
-    ts(T.ncb[:], T.l29[:], 256.0, A.mult, ["l29"], ["ncb"])
-    ts(T.maskP[:], T.c15i[:], T.p15[:], A.is_equal, ["c15i", "p15"], ["maskP"])
-
-    XB = (2, 3, 0, 1, 7, 2, 3, 0)
-
-    def x_heir(k):
-        bk = "b%d" % XB[k]
-        mm(T[bk][:], T.WH[:, 128 * k:128 * k + 128], T.Hs[:], True, False, ["WH%d" % k, "Hs"], [bk])
-
-    def x_book(k):
-        bk = "b%d" % XB[k]
+    def n_book(k):
         wk = "Wk%d" % (0 if k < 3 else 1 if k < 5 else 2 if k < 7 else 3)
-        mm(T[bk][:], T.WN[:], T.W[:, 512 * k:512 * k + 512], False, True, ["WN", wk], [bk])
+        mm(b[0][0:64, :], T.WNK[:, 64 * k:64 * k + 64], T.W[:, 512 * k:512 * k + 512], k == 0, k == 7, ["WNK", wk], ["b0"])
 
-    def x_copy(k):
-        bk = "b%d" % XB[k]
-        if k in VCOPY:
-            ts(T.HN[:, 512 * k:512 * k + 512], T[bk][:], T.cb[:], A.add, [bk, "cb"], ["HN%d" % k])
-        else:
-            act(T.HN[:, 512 * k:512 * k + 512], T[bk][:], [bk, "cb"], ["HN%d" % k], func=F.Identity, bias=T.cb[:])
+    def row(r, buf, key):
+        op("y", lambda: g.sync.dma_start(out=T.HN[r:128:16, 0:4096], in_=T[buf][:]), [buf] + FK, [key], "d_" + key[2:] + "r", 16)
 
-    CUT = (0, 256, 512, 1280)
+    def indices(t):
+        lo, hi = 256 * t, 256 * t + 256
+        ts(T.ib[:, lo:hi], T.dI[:, lo:hi], BIAS, A.subtract, ["daI", "dbI"], ["ib%d" % t])
 
-    def indices(k, what="ab"):
-        lo, hi = CUT[k], CUT[k + 1]
-        if "a" in what:
-            ts(T.ab[:, lo:hi], T.daI[:, lo:hi], BIAS, A.subtract, ["daI"], ["ab%d" % k])
-        if "b" in what:
-            ts(T.bb[:, lo:hi], T.dbI[:, lo:hi], BIAS, A.subtract, ["dbI"], ["bb%d" % k])
+    def an_t(t):
+        lo, hi = 256 * t, 256 * t + 256
+        mm(b[4][:, 0:256], T.EA[:], T.ib[:, lo:hi], True, True, ["EA", "ib%d" % t], ["b4"])
+        mm(b[4][:, 256:512], T.EB[:], T.ib[:, lo:hi], True, True, ["EB", "ib%d" % t], ["b4"])
 
-    indices(0)
-    ts(T.ownH[:], T.ownI[:], BIAS, A.subtract, ["ownI"], ["ownH"])
-
-    AK = {0: 1, 1: 2, 3: 3}
-    AR = [(0, 256), (256, 512), (512, 1024), (1024, 1280)]
-
-    def rng(t):
-        return (0, 1, 2, 2, 3)[t]
-
-    def an_t(k):
-        lo, hi = AR[k]
-        w = hi - lo
-        kk = str(min(k, 2))
-        mm(b[5][:, 0:w], T.E8[:], T.ab[:, lo:hi], True, True, ["E8", "ab" + kk], ["b5"])
-        mm(b[6][:, 0:w], T.E8[:], T.bb[:, lo:hi], True, False, ["E8", "bb" + kk], ["b6"])
-        mm(b[6][:, 0:w], T.nE8[:], T.ab[:, lo:hi], False, True, ["nE8", "ab" + kk], ["b6"])
-
-    def an_s(k):
-        lo, hi = AR[k]
-        act(T.AN[:, lo:hi], b[5][:, 0:hi - lo], ["b5"], ["AN%d" % k])
-        act(T.BA[:, lo:hi], b[6][:, 0:hi - lo], ["b6"], ["BA%d" % k])
-
-    def prep_bank(t):
-        return "b4" if t == 0 else "b7"
+    def an_s(t):
+        act(T.AN[:, 256 * t:256 * t + 256], b[4][:, 0:256], ["b4"], ["AN%d" % t])
 
     def prep_t(t):
-        kk = str(min(t, 2))
         lk = "lm%d" % (t % n)
-        bk = prep_bank(t)
-        mm(T[bk][:, 0:256], T.WN[:], T[lk][:], True, False, ["WN", lk], [bk])
-        mm(T[bk][:, 0:256], T.E01[:], T.bb[:, 256 * t:256 * t + 256], False, True, ["E01", "bb" + kk], [bk])
+        mm(b[7][:, 0:256], T.WN[:], T[lk][:], True, False, ["WN", lk], ["b7"])
+        mm(b[7][:, 0:256], T.E0[:], T.ib[:, 256 * t:256 * t + 256], False, True, ["E0", "ib%d" % t], ["b7"])
         for ch in range(2):
-            mm(T[bk][:, 256 + 128 * ch:384 + 128 * ch], T.ab[:, 256 * t + 128 * ch:256 * t + 128 * ch + 128], T.E8[:], True, True,
-               ["ab" + kk, "E8"], [bk])
-
-    def prep_s(t):
-        bk = prep_bank(t)
-        act(T.Yn[:], T[bk][:, 0:256], [bk, "m1", "ncb"], ["Yn"], func=F.Identity, scale=T.m1[:], bias=T.ncb[:])
+            mm(b[7][:, 256 + 128 * ch:384 + 128 * ch], T.ib[:, 256 * t + 128 * ch:256 * t + 128 * ch + 128], T.EA[:], True, True,
+               ["ib%d" % t, "EA"], ["b7"])
 
     def prep_nh(t):
-        bk = prep_bank(t)
-        tt(T["NH%d" % (t % 2)][:], T[bk][:, 0:256], T.Yn[:], A.subtract, [bk, "Yn"], ["NH%d" % (t % 2)])
+        k = "NH%d" % (t % 2)
+        act(T[k][:], b[7][:, 0:256], ["b7", "cb"], [k], func=F.Identity, bias=T.cb[:])
 
     def prep_ma(t):
-        k, bk = "MA%d" % (t % 2), prep_bank(t)
+        k = "MA%d" % (t % 2)
         for ch in range(2):
-            tt(T[k][:, 128 * ch:128 * ch + 128], T[bk][:, 256 + 128 * ch:384 + 128 * ch], T.maskP[:], A.mult, [bk, "maskP"], [k + "c%d" % ch])
+            tt(T[k][:, 128 * ch:128 * ch + 128], b[7][:, 256 + 128 * ch:384 + 128 * ch], T.maskP[:], A.mult, ["b7", "maskP"], [k + "c%d" % ch])
 
     def rep(t, qs, who):
         k = "lm%d" % t
@@ -294,15 +231,14 @@ def rank_program(g, core, T, topo):
 
     def deeds_hit(t, ch):
         c = str(ch)
-        k = str(rng(t))
         cols = slice(256 * t + 128 * ch, 256 * t + 128 * ch + 128)
         if t:
             rk = "R%d%d" % (t, ch)
             mm(b[2 + ch][:, 0:128], T[rk][:], T.IdH[:], True, True, [rk, "IdH"], ["b%d" % (2 + ch)])
         own, ok = own_of(t, ch)
-        tt(T["HT" + c][:], own, T.AN[:, cols], A.is_equal, [ok, "AN" + k], ["HT" + c])
+        tt(T["HT" + c][:], own, T.AN[:, cols], A.is_equal, [ok, "AN%d" % t], ["HT" + c])
         mm(b[5 + ch][:, 0:128], T["HT" + c][:], T.BO[:], True, True, ["HT" + c, "BO"], ["b%d" % (5 + ch)])
-        tt(T["hb" + c][:], T["HT" + c][:], T.BA[:, cols], A.mult, ["HT" + c, "BA" + k], ["hb" + c])
+        tt(T["hb" + c][:], T["HT" + c][:], b[4][:, 256 + 128 * ch:384 + 128 * ch], A.mult, ["HT" + c, "b4"], ["hb" + c])
 
     def deeds_list(t, ch):
         c = str(ch)
@@ -332,104 +268,154 @@ def rank_program(g, core, T, topo):
         vcopy(T.W[:, 0:8192].indirect(T["LS" + c][:, 0:8]), T[l][:, loc], ["LS" + c, l], WK)
 
     def offs(ch):
-        ts(T.off[:, 128 * ch:128 * ch + 128], T["ownN%d" % ch][:], BIAS, A.add, ["ownN%d" % ch], ["off%d" % ch])
+        ts(T.off0[:, 128 * ch:128 * ch + 128], T["ownN%d" % ch][:], BIAS, A.add, ["ownN%d" % ch], ["off0%d" % ch])
 
-    def gv(t, ch, lo, hi):
+    parts = {}
+
+    def gv(t, p, ch, lo, hi):
         a, z = 128 * ch + lo, 128 * ch + hi
-        m, l = "M%d" % ch, "lr%d" % (t % n)
-        op("v", lambda: g.vector.tensor_tensor(out=T[m][:, 16 * lo:16 * hi], in0=T.W[:, 0:4096].indirect(T.off[:, a:z]),
+        m, l, o = "M%d%d" % (p, ch), "lr%d" % (t % n), "off%d" % p
+        key = m + "_%d" % lo
+        if lo == 0:
+            parts[m] = []
+        parts[m].append(key)
+        op("v", lambda: g.vector.tensor_tensor(out=T[m][:, 16 * lo:16 * hi], in0=T.W[:, 0:4096].indirect(T[o][:, a:z]),
                                                in1=T[l][:, 16 * a:16 * z], op=A.max),
-           WK + ["off%d" % ch] + [l + "_%d" % q for q in range(16)], [m + "_%d" % lo])
+           WK + [o + str(ch)] + [l + "_%d" % q for q in range(16)], [key])
 
-    def gs(ch, lo, hi):
+    def gs(p, ch, lo, hi):
         a, z = 128 * ch + lo, 128 * ch + hi
-        act(T["H%d" % ch][:, 16 * lo:16 * hi], T.HN[:, 0:4096].indirect(T.off[:, a:z]), HK + ["off%d" % ch], ["H%d_%d" % (ch, lo)])
+        h, o = "H%d%d" % (p, ch), "off%d" % p
+        key = h + "_%d" % lo
+        if lo == 0:
+            parts[h] = []
+        parts[h].append(key)
+        act(T[h][:, 16 * lo:16 * hi], T.HN[:, 0:4096].indirect(T[o][:, a:z]), HK + [o + str(ch)], [key], bias=-float(BIAS))
 
-    MK = {c: ["M%d_0" % c, "M%d_%d" % (c, VS)] for c in (0, 1)}
-    HHK = {c: ["H%d_0" % c, "H%d_%d" % (c, SS)] for c in (0, 1)}
+    def bank(p, ch):
+        return (0, 1, 5, 6)[2 * p + ch]
 
-    def gather_whole(t, ch):
-        gv(t, ch, 0, 128)
-        wr[MK[ch][1]] = dict(wr[MK[ch][0]])
-        gs(ch, 0, 128)
-        wr[HHK[ch][1]] = dict(wr[HHK[ch][0]])
-
-    def init(t, ch, p):
-        l, bk = "lm%d" % (t % n), "b%d" % ch
-        mm(b[ch][:, 0:128], T[l][:, 128 * ch:128 * ch + 128], T.nBO[:], True, False, [l, "nBO"], [bk])
+    def init(t, p, ch):
+        l, k = "lm%d" % (t % n), bank(p, ch)
+        bk = "b%d" % k
+        mm(b[k][:, 0:128], T[l][:, 128 * ch:128 * ch + 128], T.nBO[:], True, False, [l, "nBO"], [bk])
         if p == 0:
-            mm(b[ch][:, 128:384], T["ownN%d" % ch][:], T.HI2[:], False, False, ["ownN%d" % ch, "HI2"], [bk])
+            mm(b[k][:, 128:384], T["ownN%d" % ch][:], T.nIdH[:], False, False, ["ownN%d" % ch, "nIdH"], [bk])
         else:
-            for k in (1, 2):
-                mm(b[ch][:, 128 * k:128 * k + 128], T.HI2[:, 0:128], T["OT%d" % ch][:], False, False, ["HI2", "OT%d" % ch], [bk])
+            mm(b[k][:, 128:256], T.nIdH[:, 0:128], T["Hc%d" % ch][:], False, False, ["nIdH", "Hc%d" % ch], [bk])
 
-    def sums(ch):
+    def sums_h(p, ch):
+        k, h, w = bank(p, ch), "H%d%d" % (p, ch), (24, 16)[p]
         for q in range(16):
-            mm(b[ch][:, q:384:16], T["H%d" % ch][:, q:2048:16], T.RH[:], False, False, HHK[ch] + ["RH"], ["b%d" % ch])
-        for q in range(16):
-            mm(b[ch][:, q:128:16], T["M%d" % ch][:, q:2048:16], T.RM[:], False, q == 15, MK[ch] + ["RM"], ["b%d" % ch])
+            mm(b[k][:, q:16 * w:16], T[h][:, q:2048:16], T.RH[:, 0:w], False, False, parts[h] + ["RH"], ["b%d" % k])
 
-    def sign(ch):
-        act(T["SG%d" % ch][:], b[ch][:, 0:128], ["b%d" % ch], ["SG%d" % ch], func=F.Sign, bias=-TH)
+    def sums_m(p, ch):
+        k, m = bank(p, ch), "M%d%d" % (p, ch)
+        for q in range(16):
+            mm(b[k][:, q:128:16], T[m][:, q:2048:16], T.RM[:], False, q == 15, parts[m] + ["RM"], ["b%d" % k])
+
+    def stay_v(ch):
+        k, c = bank(0, ch), "n%d" % ch
+        ts(T[c][:], b[k][:, 0:128], TH, A.is_ge, ["b%d" % k], [c])
+
+    def stay_s(ch):
+        k, c = bank(0, ch), "n%d" % ch
+        act(T[c][:], b[k][:, 0:128], ["b%d" % k], [c], func=F.Sigmoid, scale=KS, bias=-KS * TH)
+
+    def stay_t(ch):
+        k, c = bank(1, ch), "n%d" % ch
+        mm(b[k][:, 0:128], T.BI[:], T[c][:], False, False, ["BI", c], ["b%d" % k])
+
+    def move(ch):
+        k, c = bank(1, ch), "m%d" % ch
+        act(T[c][:], b[k][:, 0:128], ["b%d" % k], [c], func=F.Sigmoid, scale=-KS, bias=KS * TH)
+
+    def copy_h(ch):
+        k, c = bank(0, ch), "Hc%d" % ch
+        act(T[c][:], b[k][:, 256:384], ["b%d" % k], [c])
+
+    def first(ch):
+        k, c = bank(0, ch), str(ch)
+        bk = "b%d" % k
+        tt(T["tt" + c][:], T["n" + c][:], b[k][:, 128:256], A.mult, ["n" + c, bk], ["tt" + c])
+        tt(T["XX" + c][:], b[k][:, 256:384], T["tt" + c][:], A.subtract, [bk, "tt" + c], ["XX" + c])
+
+    def first_t(ch):
+        c = str(ch)
+        mm(b[2 + ch][:, 0:128], T.IdH[:], T["XX" + c][:], True, True, ["IdH", "XX" + c], ["b%d" % (2 + ch)])
 
     def upd(ch, dst):
-        c = str(ch)
-        tt(T["tt" + c][:], T["SG" + c][:], b[ch][:, 128:256], A.mult, ["SG" + c, "b" + c], ["tt" + c])
-        tt(T[dst][:], b[ch][:, 256:384], T["tt" + c][:], A.add, ["b" + c, "tt" + c], [dst])
+        k, c = bank(1, ch), str(ch)
+        tt(T["tt" + c][:], T["m" + c][:], b[k][:, 128:256], A.mult, ["m" + c, "b%d" % k], ["tt" + c])
+        tt(T[dst][:], b[2 + ch][:, 0:128], T["tt" + c][:], A.add, ["b%d" % (2 + ch), "tt" + c], [dst])
 
     def turn(ch, src):
         mm(b[2 + ch][:, 0:128], T[src][:], T.IdH[:], True, True, [src, "IdH"], ["b%d" % (2 + ch)])
 
     def conv(ch):
-        ts(T.off[:, 128 * ch:128 * ch + 128], b[2 + ch][:, 0:128], BIAS, A.add, ["b%d" % (2 + ch)], ["off%d" % ch])
+        ts(T.off1[:, 128 * ch:128 * ch + 128], b[2 + ch][:, 0:128], BIAS, A.add, ["b%d" % (2 + ch)], ["off1%d" % ch])
 
-    act(T.nBO[:], T.BO[:], ["BO"], ["nBO"], scale=-1.0)
-    act(T.RM[:], T.BO[:, 0:128:16], ["BO"], ["RM"], scale=2.0)
-    act(T.K4[:], T.BO[:, 0:128:16], ["BO"], ["K4"], scale=4096.0)
-    for k in (0, 1):
-        x_heir(k)
+    ts(T.EA[:], T.e8i[:], 0, A.is_equal, ["e8i"], ["EA"])
+    op("v", lambda: g.vector.memset(T.WN[:], 0.0), [], ["WN"])
+    op("v", lambda: g.vector.memset(T.WNK[:], 0.0), [], ["WNK"])
+    op("v", lambda: g.vector.memset(T.HN[:, 0:1024], 0.0), [], FK[0:2])
+    mm(b[5][:, 0:128], T.EA[:], T.EA[:], True, True, ["EA"], ["b5"])
+    act(T.BO[:], b[5][:, 0:128], ["b5"], ["BO"])
+    act(T.WN[:, 1:128:16], b[5][:, 0:128:16], ["b5"], ["WN"])
+    for k in range(8):
+        act(T.WNK[:, 65 * k:64 * k + 64:8], b[5][:, 0:128:16], ["b5"], ["WNK"])
+    act(T.nBO[:], b[5][:, 0:128], ["b5"], ["nBO"], scale=-1.0)
+    act(T.HN[:, 1024:2048], T.HN[:, 0:1024], FK[0:2], FK[2:4])
+    ts(T.EN[:], T.e8i[:], 0, A.is_equal, ["e8i"], ["EN"], -1.0, A.mult)
+    ts(T.EP[:], T.e8i[:], -8, A.is_equal, ["e8i"], ["EP"])
+    tt(T.EB[:], T.EP[:], T.EN[:], A.add, ["EP", "EN"], ["EB"])
+    ts(T.E16[:], T.e16i[:], 0, A.is_equal, ["e16i"], ["E16"])
+    mm(b[6][:, 0:128], T.E16[:], T.E16[:], True, True, ["E16"], ["b6"])
+    act(T.maskP[:], b[6][:, 0:128], ["b6"], ["maskP"], func=F.Sigmoid, scale=2 * KS, bias=-KS)
+    indices(0)
     an_t(0)
     an_s(0)
+    act(T.HN[:, 2048:2560], T.HN[:, 0:512], FK[0:1], FK[4:5])
+    vcopy(T.Hf[:], T.heirI[:], ["heirI"], ["Hf"])
+    row(0, "Hf", "HNh")
+    ts(T.E0[:], T.e0i[:], 0, A.is_equal, ["e0i"], ["E0"])
     prep_t(0)
-    prep_s(0)
-    for k in (2, 3, 4):
-        x_heir(k)
-    ts(T.K1[:], T.BO[:, 0:128:16], 1.0, A.mult, ["BO"], ["K1"])
-    indices(1)
-    prep_ma(0)
+    ts(T.cb[:], T.maskP[:, 0:1], float(BIAS), A.mult, ["maskP"], ["cb"])
     prep_nh(0)
-    for k in (0, 1, 2):
-        x_book(k)
-    rep(0, range(6), "s")
-    x_copy(0)
+    ts(T.ownH[:], T.ownI[:], BIAS, A.subtract, ["ownI"], ["ownH"])
+    prep_ma(0)
+    ts(T.K1[:], T.BO[:, 0:128:16], 1.0, A.mult, ["BO"], ["K1"])
+    act(T.K4[:], T.BO[:, 0:128:16], ["BO"], ["K4"], scale=4096.0)
+    act(T.RM[:], T.BO[:, 0:128:16], ["BO"], ["RM"], scale=2.0)
+    for k in range(N0):
+        n_book(k)
     deeds_hit(0, 0)
     deeds_hit(0, 1)
-    x_heir(5)
-    x_copy(1)
-    x_copy(2)
-    ts(T.HI2[:, 0:128], T.ci[:], T.pf[:], A.is_equal, ["ci", "pf"], ["HI2"], 0.5, A.mult)
-    ts(T.HI2[:, 128:256], T.ci[:], T.pf[:], A.is_equal, ["ci", "pf"], ["HI2"], 0.5, A.mult)
     deeds_list(0, 0)
     deeds_list(0, 1)
-    x_heir(6)
-    x_heir(7)
-    rep(0, range(6, 16 - VR0), "s")
-    ts(T.RH[:, 0:8], T.BO[:, 0:128:16], T.l29[:], A.mult, ["BO", "l29"], ["RH"], -1.0, A.mult)
-    ts(T.RH[:, 8:16], T.BO[:, 0:128:16], T.l01[:], A.mult, ["BO", "l01"], ["RH"], -0.5, A.mult)
-    ts(T.RH[:, 16:24], T.BO[:, 0:128:16], T.l01[:], A.mult, ["BO", "l01"], ["RH"], 0.5, A.mult)
-    ts(T.IdH[:], T.ci[:], T.pf[:], A.is_equal, ["ci", "pf"], ["IdH"])
-    offs(0)
-    offs(1)
+    rep(0, range(0, S0), "s")
+    for k in range(N0, 7):
+        n_book(k)
     deeds_end(0)
     deeds_end(1)
-    for k in range(3, 8):
-        x_book(k)
-        x_copy(k)
-    rep(0, range(16 - VR0, 16), "v")
+    offs(0)
+    offs(1)
+    ts(T.IdH[:], T.D0[:], 0, A.is_equal, ["D0"], ["IdH"])
+    ts(T.nIdH[:, 0:128], T.D0[:], 0, A.is_equal, ["D0"], ["nIdH"], -1.0, A.mult)
+    ts(T.nIdH[:, 128:256], T.D0[:], 0, A.mult, ["D0"], ["nIdH"])
+    ts(T.BI[:], T.D0[:], 0, A.is_equal, ["D0"], ["BI"], float(BIG), A.mult)
+    ts(T.RH[:, 0:8], T.V8[:], -1, A.is_equal, ["V8"], ["RH"], -1.0, A.mult)
+    for k in (1, 2):
+        ts(T.RH[:, 8 * k:8 * k + 8], T.V8[:], 0, A.is_equal, ["V8"], ["RH"])
+    indices(1)
+    rep(0, range(S0, 16), "v")
+    n_book(7)
+    act(T.NS[:], b[0][0:64, :], ["b0"], ["NS"])
+    row(1, "NS", "HNn")
     scatter_w(0, 0)
+    scatter_w(0, 1)
     scatter_h(0, 0)
     scatter_h(0, 1)
-    scatter_w(0, 1)
 
     nxt = T.cores[(rank + 1) % n]
     prv = T.cores[(rank - 1) % n]
@@ -439,8 +425,17 @@ def rank_program(g, core, T, topo):
 
     def out_yo(ch):
         loc = slice(128 * ch, 128 * ch + 128)
+        turn(ch, "OT%d" % ch)
         ts(T.yof[:, loc], b[2 + ch][:, 0:128], float(BIAS), A.add, ["b%d" % (2 + ch)], ["yof%d" % ch])
         op("y", lambda: g.sync.dma_start(out=T.yo[:, loc], in_=T.yof[:, loc]), ["yof%d" % ch], [], "dout", 16)
+
+    def done(t, ch):
+        if t == R - 1:
+            upd(ch, "OT%d" % ch)
+        else:
+            dst = "SD%d%d" % (t, ch)
+            upd(ch, dst)
+            send(nxt, T["R%d%d" % (t + 1, ch)][:], T[dst][:], "r%d%d" % (t + 1, ch), dst)
 
     for t in range(R):
         last = t == R - 1
@@ -451,75 +446,75 @@ def rank_program(g, core, T, topo):
                 if ch == 0:
                     offs(0)
                 deeds_end(ch)
+                if ch == 1:
+                    offs(1)
                 scatter_h(t, ch)
                 scatter_w(t, ch)
         init(t, 0, 0)
-        init(t, 1, 0)
+        init(t, 0, 1)
         if not last:
             prep_t(t + 1)
-        if t in AK:
-            an_t(AK[t])
-        gather_whole(t, 0)
-        if t:
-            offs(1)
+            an_t(t + 1)
+        gs(0, 0, 0, 128)
+        gv(t, 0, 0, 0, 128)
         if last:
-            for k, lane in (("yha", 0), ("yhb", 1)):
-                op("y", lambda: g.sync.dma_start(out=T[k][:], in_=T.HN[lane:128:16, 0:4096]), HK, [k], "d_" + k, 16)
+            op("y", lambda: g.sync.dma_start(out=T.yh[:], in_=T.HN[0:128:16, 0:4096]), HK, [], "dout", 16)
             op("y", lambda: g.sync.dma_start(out=T.yd[:], in_=T.W[:, 0:4096]), WK, [], "dout", 16)
-        sums(0)
-        gv(t, 1, 0, VS)
-        gs(1, 0, SS)
-        sign(0)
-        gs(1, SS, 128)
-        upd(0, "OT0")
-        turn(0, "OT0")
-        init(t, 0, 1)
-        gv(t, 1, VS, 128)
+        sums_h(0, 0)
+        sums_m(0, 0)
+        gs(0, 1, 0, SA)
+        copy_h(0)
+        gs(0, 1, SA, 128)
+        turn(0, "Hc0")
+        init(t, 1, 0)
+        gv(t, 0, 1, 0, VA)
         conv(0)
-        sums(1)
-        gv(t, 0, 0, VS)
-        gs(0, 0, SS)
-        sign(1)
-        gs(0, SS, 128)
-        if last:
-            act(T.yh2[:], T.yha[:], ["yha"], ["yh2"], bias=float(BIAS))
-        upd(1, "OT1")
-        turn(1, "OT1")
-        conv(1)
+        gv(t, 0, 1, VA, 128)
+        sums_h(0, 1)
+        sums_m(0, 1)
+        gs(1, 0, 0, SB)
+        copy_h(1)
+        gs(1, 0, SB, 128)
+        turn(1, "Hc1")
         init(t, 1, 1)
-        gv(t, 0, VS, 128)
-        sums(0)
-        gather_whole(t, 1)
-        sign(0)
-        sums(1)
+        gv(t, 1, 0, 0, VB)
+        conv(1)
+        gv(t, 1, 0, VB, 128)
+        stay_v(0)
+        first(0)
+        sums_h(1, 0)
+        stay_t(0)
+        sums_m(1, 0)
+        first_t(0)
+        gs(1, 1, 0, 128)
+        stay_s(1)
+        gv(t, 1, 1, 0, VC)
+        move(0)
+        done(t, 0)
+        gv(t, 1, 1, VC, 128)
+        sums_h(1, 1)
+        stay_t(1)
+        if last:
+            out_yo(0)
+        sums_m(1, 1)
+        first(1)
+        first_t(1)
         if not last:
-            upd(0, "SD%d0" % t)
-            send(nxt, T["R%d0" % (t + 1)][:], T["SD%d0" % t][:], "r%d0" % (t + 1), "SD%d0" % t)
-            prep_s(t + 1)
-            if t in AK:
-                an_s(AK[t])
             prep_ma(t + 1)
-            if t == 0:
-                indices(2, "a")
-            sign(1)
-            upd(1, "SD%d1" % t)
-            send(nxt, T["R%d1" % (t + 1)][:], T["SD%d1" % t][:], "r%d1" % (t + 1), "SD%d1" % t)
+            if t + 2 < R:
+                indices(t + 2)
+            an_s(t + 1)
+            if t + 1 < n:
+                rep(t + 1, range(0, RB), "s")
+                rep(t + 1, range(16 - VR, 16), "v")
+        move(1)
+        done(t, 1)
+        if last:
+            out_yo(1)
+        else:
             prep_nh(t + 1)
             if t + 1 < n:
-                rep(t + 1, range(16 - VR, 16), "v")
-                rep(t + 1, range(16 - VR), "s")
-            if t == 0:
-                indices(2, "b")
-        else:
-            tt(T.yhf[:], T.yh2[:], T.yhb[:], A.add, ["yh2", "yhb"], ["yhf"])
-            op("y", lambda: g.sync.dma_start(out=T.yh[:], in_=T.yhf[:]), ["yhf"], [], "dout", 16)
-            upd(0, "OT0")
-            turn(0, "OT0")
-            out_yo(0)
-            sign(1)
-            upd(1, "OT1")
-            turn(1, "OT1")
-            out_yo(1)
+                rep(t + 1, range(RB, 16 - VR), "s")
 
     g.sync.wait_ge(T.sem.dout, cnt["dout"])
     wait("p", {s: c for s, c in cnt.items() if s != "dout"})

from concourse.mybir import AluOpType as A, ActivationFunctionType as F

BIAS = 2048
TH = 136.5 + 2048
BIG = 8192
KS = 256.0
R = 5
VA, VB, VC, SA, SB = 112, 112, 112, 104, 104
S0, VR, RB = 10, 2, 3
N0 = 5

SCRATCH = {}
SEMAPHORES = ["v", "s", "t", "p", "loc", "dout"]


def _buf(name, cols, dtype, where="sbuf", rows=128):
    SCRATCH[name] = (where, [rows, cols], dtype)


_buf("D0", 128, "int32")
_buf("V8", 8, "int32")
_buf("NS", 512, "float32", rows=64)
_buf("Hf", 512, "float32", rows=64)
_buf("ownI", 256, "int32")
for _n, _c, _r in (("e8i", 128, 16), ("e0i", 128, 16), ("e16i", 128, 16), ("heirI", 512, 64), ("dI", 1280, 16)):
    _buf(_n, _c, "int32", rows=_r)
for _n, _c in (("cb", 1), ("NH0", 256), ("NH1", 256), ("AN", 1280), ("hb0", 128), ("hb1", 128),
               ("tt0", 128), ("tt1", 128), ("yof", 256), ("HN", 8192)):
    _buf(_n, _c, "float32")
for _n, _c in (("BO", 128), ("nBO", 128), ("maskP", 128), ("RM", 8), ("K4", 8), ("BI", 128), ("WN", 128), ("WNK", 512),
               ("W", 8192), ("M00", 2048), ("M01", 2048), ("M10", 2048), ("M11", 2048),
               ("HT0", 128), ("HT1", 128), ("X0", 128), ("X1", 128), ("n0", 128), ("n1", 128), ("m0", 128), ("m1", 128),
               ("lm0", 256), ("lm1", 256), ("lm2", 256), ("lm3", 256),
               ("lr0", 4096), ("lr1", 4096), ("lr2", 4096), ("lr3", 4096)):
    _buf(_n, _c, "bfloat16")
for _n, _c in (("EA", 128), ("EP", 128), ("EN", 128), ("EB", 128), ("E0", 128), ("E16", 128), ("ib", 1280)):
    _buf(_n, _c, "float16", rows=16)
for _n, _c in (("IdH", 128), ("nIdH", 256), ("RH", 24), ("K1", 8), ("ownH", 256), ("MA0", 256), ("MA1", 256),
               ("ownN0", 128), ("ownN1", 128), ("Hc0", 128), ("Hc1", 128), ("XX0", 128), ("XX1", 128),
               ("OT0", 128), ("OT1", 128), ("H00", 2048), ("H01", 2048), ("H10", 2048), ("H11", 2048)):
    _buf(_n, _c, "float16")
_buf("off0", 256, "uint16")
_buf("off1", 256, "uint16")
_buf("LS0", 8, "uint16")
_buf("LS1", 8, "uint16")
for _t in range(4):
    for _c in range(2):
        _buf("SD%d%d" % (_t, _c), 128, "float16")
        _buf("R%d%d" % (_t + 1, _c), 128, "float16")
        SEMAPHORES.append("r%d%d" % (_t + 1, _c))
for _t in (1, 2, 3):
    SEMAPHORES.append("l%d" % _t)
for _n in ("own", "lm", "heir", "da", "db", "bk0", "bk1", "bk2", "bk3", "hr", "nr"):
    SEMAPHORES.append("d_" + _n)
for _k in range(8):
    _buf("b%d" % _k, 512, "float32", "psum")
BANKS = ["b%d" % _k for _k in range(8)]


def rank_program(g, core, T, topo):
    rank = T.rank_of(core)
    if rank is None:
        return
    n = len(T.cores)
    eng = {"v": g.vector, "s": g.scalar, "t": g.tensor, "p": g, "y": g.sync}
    know = {q: {} for q in eng}
    cnt = {}
    snap = {}
    wr, rd, acc = {}, {}, {}

    def wait(q, deps):
        todo = {s: c for s, c in deps.items() if know[q].get(s, 0) < c}
        for s, c in sorted(todo.items()):
            if any(o != s and snap.get((o, oc), {}).get(s, 0) >= c for o, oc in todo.items()):
                continue
            eng[q].wait_ge(T.sem[s], c)
        for s, c in todo.items():
            for s2, c2 in snap.get((s, c), {}).items():
                know[q][s2] = max(know[q].get(s2, 0), c2)
            know[q][s] = max(know[q].get(s, 0), c)

    def deps_of(q, reads, writes):
        d = {}

        def put(src, skip=None):
            for s, c in src.items():
                if s != skip:
                    d[s] = max(d.get(s, 0), c)
        for k in list(reads) + list(writes):
            if k in BANKS:
                put(acc.get(k, {}), q)
            else:
                put(wr.get(k, {}))
        for k in writes:
            if k not in BANKS:
                put(rd.get(k, {}))
        return d

    def note(q, sem, inc, reads, writes):
        cnt[sem] = cnt.get(sem, 0) + inc
        c = cnt[sem]
        snap[(sem, c)] = dict(know[q])
        for k in list(reads) + list(writes):
            if k in BANKS:
                acc.setdefault(k, {})[sem] = c
        for k in reads:
            if k not in BANKS:
                rd.setdefault(k, {})[sem] = c
        for k in writes:
            if k not in BANKS:
                wr[k] = {sem: c}
                rd[k] = {}

    def op(q, fn, reads, writes, sem=None, inc=1):
        wait(q, deps_of(q, reads, writes))
        sem = sem or q
        fn().then_inc(T.sem[sem], inc)
        note(q, sem, inc, reads, writes)

    def ts(out, in0, s1, op0, reads, writes, s2=None, op1=None):
        if op1 is None:
            op("v", lambda: g.vector.tensor_scalar(out=out, in0=in0, scalar1=s1, scalar2=None, op0=op0), reads, writes)
        else:
            op("v", lambda: g.vector.tensor_scalar(out=out, in0=in0, scalar1=s1, scalar2=s2, op0=op0, op1=op1), reads, writes)

    def tt(out, in0, in1, o, reads, writes):
        op("v", lambda: g.vector.tensor_tensor(out=out, in0=in0, in1=in1, op=o), reads, writes)

    def vcopy(out, in_, reads, writes):
        op("v", lambda: g.vector.tensor_copy(out=out, in_=in_), reads, writes)

    def act(out, in_, reads, writes, func=F.Copy, **kw):
        op("s", lambda: g.scalar.activation(out=out, in_=in_, func=func, **kw), reads, writes)

    def mm(out, lhsT, rhs, start, stop, reads, writes):
        op("t", lambda: g.tensor.matmul(out=out, lhsT=lhsT, rhs=rhs, start=start, stop=stop), reads, writes)

    def iota(name, pattern, base, cm):
        op("p", lambda: g.iota(T[name][:], pattern, base, cm), [], [name])

    def load(q, out, in_, sem, key):
        op(q, lambda: eng[q].dma_start(out=out, in_=in_), [], [key], sem, 16)

    b = [T[k] for k in BANKS]

    load("s", T.heirI[:], T.heir[:], "d_heir", "heirI")
    load("y", T.dI[0:8, :], T.da[:], "d_da", "daI")
    load("s", T.dI[8:16, :], T.db[:], "d_db", "dbI")
    load("y", T.lm0[:], T.lm[:], "d_lm", "lm0")
    load("y", T.ownI[:], T.own[:], "d_own", "ownI")
    PIECE = (0, 1536, 2560, 3584, 4096)
    for k in range(4):
        lo, hi = PIECE[k], PIECE[k + 1]
        load("s" if k % 2 == 0 else "y", T.W[:, lo:hi], T.bk[:, lo:hi], "d_bk%d" % k, "Wk%d" % k)
    WK = ["Wk%d" % k for k in range(4)]
    FK = ["HN%d" % k for k in range(8)]
    HK = FK + ["HNh", "HNn"]

    iota("e8i", [[1, 8], [0, 16]], 0, -1)
    iota("e16i", [[0, 8], [1, 16]], 0, -1)
    iota("e0i", [[1, 128]], 128, -16)
    iota("D0", [[1, 128]], 0, -1)
    iota("V8", [[16, 8]], 0, -1)
    op("p", lambda: g.iota(T.HN[:, 2560:4096], [[0, 1536]], 0, 0, allow_small_or_imprecise_dtypes=True), [], FK[5:])

    def send(dst, out, in_, sem, key):
        wait("p", deps_of("p", [key], []))
        rid, pid, _ = topo.addr(dst)
        ne = len(topo.engines(core, dst))
        g.remote_dma(out, in_, T.sem[sem], T.sem.loc, pid, rid, topo.mask(core, dst))
        cnt["loc"] = cnt.get("loc", 0) + ne

    def arrive(sem, key, src):
        ne = len(topo.engines(src, core))
        cnt[sem] = ne
        wr[key] = {sem: ne}
        rd[key] = {}

    for t in (1, 2, 3):
        send(T.cores[(rank + t) % n], T["lm%d" % t][:], T.lm0[:], "l%d" % t, "lm0")
        arrive("l%d" % t, "lm%d" % t, T.cores[(rank - t) % n])

    def n_book(k):
        wk = "Wk%d" % (0 if k < 3 else 1 if k < 5 else 2 if k < 7 else 3)
        mm(b[0][0:64, :], T.WNK[:, 64 * k:64 * k + 64], T.W[:, 512 * k:512 * k + 512], k == 0, k == 7, ["WNK", wk], ["b0"])

    def row(r, buf, key):
        op("y", lambda: g.sync.dma_start(out=T.HN[r:128:16, 0:4096], in_=T[buf][:]), [buf] + FK, [key], "d_" + key[2:] + "r", 16)

    def indices(t):
        lo, hi = 256 * t, 256 * t + 256
        ts(T.ib[:, lo:hi], T.dI[:, lo:hi], BIAS, A.subtract, ["daI", "dbI"], ["ib%d" % t])

    def an_t(t):
        lo, hi = 256 * t, 256 * t + 256
        mm(b[4][:, 0:256], T.EA[:], T.ib[:, lo:hi], True, True, ["EA", "ib%d" % t], ["b4"])
        mm(b[4][:, 256:512], T.EB[:], T.ib[:, lo:hi], True, True, ["EB", "ib%d" % t], ["b4"])

    def an_s(t):
        act(T.AN[:, 256 * t:256 * t + 256], b[4][:, 0:256], ["b4"], ["AN%d" % t])

    def prep_t(t):
        lk = "lm%d" % (t % n)
        mm(b[7][:, 0:256], T.WN[:], T[lk][:], True, False, ["WN", lk], ["b7"])
        mm(b[7][:, 0:256], T.E0[:], T.ib[:, 256 * t:256 * t + 256], False, True, ["E0", "ib%d" % t], ["b7"])
        for ch in range(2):
            mm(b[7][:, 256 + 128 * ch:384 + 128 * ch], T.ib[:, 256 * t + 128 * ch:256 * t + 128 * ch + 128], T.EA[:], True, True,
               ["ib%d" % t, "EA"], ["b7"])

    def prep_nh(t):
        k = "NH%d" % (t % 2)
        act(T[k][:], b[7][:, 0:256], ["b7", "cb"], [k], func=F.Identity, bias=T.cb[:])

    def prep_ma(t):
        k = "MA%d" % (t % 2)
        for ch in range(2):
            tt(T[k][:, 128 * ch:128 * ch + 128], b[7][:, 256 + 128 * ch:384 + 128 * ch], T.maskP[:], A.mult, ["b7", "maskP"], [k + "c%d" % ch])

    def rep(t, qs, who):
        k = "lm%d" % t
        for q in qs:
            if who == "v":
                vcopy(T["lr%d" % t][:, q:4096:16], T[k][:], [k], ["lr%d_%d" % (t, q)])
            else:
                act(T["lr%d" % t][:, q:4096:16], T[k][:], [k], ["lr%d_%d" % (t, q)])

    def own_of(t, ch):
        if t == 0:
            return T.ownH[:, 128 * ch:128 * ch + 128], "ownH"
        return b[2 + ch][:, 0:128], "b%d" % (2 + ch)

    def deeds_hit(t, ch):
        c = str(ch)
        cols = slice(256 * t + 128 * ch, 256 * t + 128 * ch + 128)
        if t:
            rk = "R%d%d" % (t, ch)
            mm(b[2 + ch][:, 0:128], T[rk][:], T.IdH[:], True, True, [rk, "IdH"], ["b%d" % (2 + ch)])
        own, ok = own_of(t, ch)
        tt(T["HT" + c][:], own, T.AN[:, cols], A.is_equal, [ok, "AN%d" % t], ["HT" + c])
        mm(b[5 + ch][:, 0:128], T["HT" + c][:], T.BO[:], True, True, ["HT" + c, "BO"], ["b%d" % (5 + ch)])
        tt(T["hb" + c][:], T["HT" + c][:], b[4][:, 256 + 128 * ch:384 + 128 * ch], A.mult, ["HT" + c, "b4"], ["hb" + c])

    def deeds_list(t, ch):
        c = str(ch)
        loc = slice(128 * ch, 128 * ch + 128)
        own, ok = own_of(t, ch)
        tt(T["X" + c][:], b[5 + ch][:, 0:128], T.maskP[:], A.min, ["b%d" % (5 + ch), "maskP"], ["X" + c])
        m = "MA%d" % (t % 2)
        lst = b[4][:, 8 * ch:8 * ch + 8]
        mm(lst, T[m][:, loc], T.K1[:], True, False, [m + "c" + c, "K1"], ["b4"])
        mm(lst, T["X" + c][:], T.K4[:], False, True, ["X" + c, "K4"], ["b4"])
        tt(T["ownN" + c][:], own, T["hb" + c][:], A.add, [ok, "hb" + c], ["ownN" + c])

    def deeds_end(ch):
        c = str(ch)
        ts(T["LS" + c][:], b[4][:, 8 * ch:8 * ch + 8], BIAS, A.add, ["b4"], ["LS" + c])

    def scatter_h(t, ch):
        c = str(ch)
        h = "NH%d" % (t % 2)
        loc = slice(128 * ch, 128 * ch + 128)
        vcopy(T.HN[:, 0:8192].indirect(T["LS" + c][:, 0:8]), T[h][:, loc], ["LS" + c, h], HK)

    def scatter_w(t, ch):
        c = str(ch)
        l = "lm%d" % (t % n)
        loc = slice(128 * ch, 128 * ch + 128)
        vcopy(T.W[:, 0:8192].indirect(T["LS" + c][:, 0:8]), T[l][:, loc], ["LS" + c, l], WK)

    def offs(ch):
        ts(T.off0[:, 128 * ch:128 * ch + 128], T["ownN%d" % ch][:], BIAS, A.add, ["ownN%d" % ch], ["off0%d" % ch])

    parts = {}

    def gv(t, p, ch, lo, hi):
        a, z = 128 * ch + lo, 128 * ch + hi
        m, l, o = "M%d%d" % (p, ch), "lr%d" % (t % n), "off%d" % p
        key = m + "_%d" % lo
        if lo == 0:
            parts[m] = []
        parts[m].append(key)
        op("v", lambda: g.vector.tensor_tensor(out=T[m][:, 16 * lo:16 * hi], in0=T.W[:, 0:4096].indirect(T[o][:, a:z]),
                                               in1=T[l][:, 16 * a:16 * z], op=A.max),
           WK + [o + str(ch)] + [l + "_%d" % q for q in range(16)], [key])

    def gs(p, ch, lo, hi):
        a, z = 128 * ch + lo, 128 * ch + hi
        h, o = "H%d%d" % (p, ch), "off%d" % p
        key = h + "_%d" % lo
        if lo == 0:
            parts[h] = []
        parts[h].append(key)
        act(T[h][:, 16 * lo:16 * hi], T.HN[:, 0:4096].indirect(T[o][:, a:z]), HK + [o + str(ch)], [key], bias=-float(BIAS))

    def bank(p, ch):
        return (0, 1, 5, 6)[2 * p + ch]

    def init(t, p, ch):
        l, k = "lm%d" % (t % n), bank(p, ch)
        bk = "b%d" % k
        mm(b[k][:, 0:128], T[l][:, 128 * ch:128 * ch + 128], T.nBO[:], True, False, [l, "nBO"], [bk])
        if p == 0:
            mm(b[k][:, 128:384], T["ownN%d" % ch][:], T.nIdH[:], False, False, ["ownN%d" % ch, "nIdH"], [bk])
        else:
            mm(b[k][:, 128:256], T.nIdH[:, 0:128], T["Hc%d" % ch][:], False, False, ["nIdH", "Hc%d" % ch], [bk])

    def sums_h(p, ch):
        k, h, w = bank(p, ch), "H%d%d" % (p, ch), (24, 16)[p]
        for q in range(16):
            mm(b[k][:, q:16 * w:16], T[h][:, q:2048:16], T.RH[:, 0:w], False, False, parts[h] + ["RH"], ["b%d" % k])

    def sums_m(p, ch):
        k, m = bank(p, ch), "M%d%d" % (p, ch)
        for q in range(16):
            mm(b[k][:, q:128:16], T[m][:, q:2048:16], T.RM[:], False, q == 15, parts[m] + ["RM"], ["b%d" % k])

    def stay_v(ch):
        k, c = bank(0, ch), "n%d" % ch
        ts(T[c][:], b[k][:, 0:128], TH, A.is_ge, ["b%d" % k], [c])

    def stay_s(ch):
        k, c = bank(0, ch), "n%d" % ch
        act(T[c][:], b[k][:, 0:128], ["b%d" % k], [c], func=F.Sigmoid, scale=KS, bias=-KS * TH)

    def stay_t(ch):
        k, c = bank(1, ch), "n%d" % ch
        mm(b[k][:, 0:128], T.BI[:], T[c][:], False, False, ["BI", c], ["b%d" % k])

    def move(ch):
        k, c = bank(1, ch), "m%d" % ch
        act(T[c][:], b[k][:, 0:128], ["b%d" % k], [c], func=F.Sigmoid, scale=-KS, bias=KS * TH)

    def copy_h(ch):
        k, c = bank(0, ch), "Hc%d" % ch
        act(T[c][:], b[k][:, 256:384], ["b%d" % k], [c])

    def first(ch):
        k, c = bank(0, ch), str(ch)
        bk = "b%d" % k
        tt(T["tt" + c][:], T["n" + c][:], b[k][:, 128:256], A.mult, ["n" + c, bk], ["tt" + c])
        tt(T["XX" + c][:], b[k][:, 256:384], T["tt" + c][:], A.subtract, [bk, "tt" + c], ["XX" + c])

    def first_t(ch):
        c = str(ch)
        mm(b[2 + ch][:, 0:128], T.IdH[:], T["XX" + c][:], True, True, ["IdH", "XX" + c], ["b%d" % (2 + ch)])

    def upd(ch, dst):
        k, c = bank(1, ch), str(ch)
        tt(T["tt" + c][:], T["m" + c][:], b[k][:, 128:256], A.mult, ["m" + c, "b%d" % k], ["tt" + c])
        tt(T[dst][:], b[2 + ch][:, 0:128], T["tt" + c][:], A.add, ["b%d" % (2 + ch), "tt" + c], [dst])

    def turn(ch, src):
        mm(b[2 + ch][:, 0:128], T[src][:], T.IdH[:], True, True, [src, "IdH"], ["b%d" % (2 + ch)])

    def conv(ch):
        ts(T.off1[:, 128 * ch:128 * ch + 128], b[2 + ch][:, 0:128], BIAS, A.add, ["b%d" % (2 + ch)], ["off1%d" % ch])

    ts(T.EA[:], T.e8i[:], 0, A.is_equal, ["e8i"], ["EA"])
    op("v", lambda: g.vector.memset(T.WN[:], 0.0), [], ["WN"])
    op("v", lambda: g.vector.memset(T.WNK[:], 0.0), [], ["WNK"])
    op("v", lambda: g.vector.memset(T.HN[:, 0:1024], 0.0), [], FK[0:2])
    mm(b[5][:, 0:128], T.EA[:], T.EA[:], True, True, ["EA"], ["b5"])
    act(T.BO[:], b[5][:, 0:128], ["b5"], ["BO"])
    act(T.WN[:, 1:128:16], b[5][:, 0:128:16], ["b5"], ["WN"])
    for k in range(8):
        act(T.WNK[:, 65 * k:64 * k + 64:8], b[5][:, 0:128:16], ["b5"], ["WNK"])
    act(T.nBO[:], b[5][:, 0:128], ["b5"], ["nBO"], scale=-1.0)
    act(T.HN[:, 1024:2048], T.HN[:, 0:1024], FK[0:2], FK[2:4])
    ts(T.EN[:], T.e8i[:], 0, A.is_equal, ["e8i"], ["EN"], -1.0, A.mult)
    ts(T.EP[:], T.e8i[:], -8, A.is_equal, ["e8i"], ["EP"])
    tt(T.EB[:], T.EP[:], T.EN[:], A.add, ["EP", "EN"], ["EB"])
    ts(T.E16[:], T.e16i[:], 0, A.is_equal, ["e16i"], ["E16"])
    mm(b[6][:, 0:128], T.E16[:], T.E16[:], True, True, ["E16"], ["b6"])
    act(T.maskP[:], b[6][:, 0:128], ["b6"], ["maskP"], func=F.Sigmoid, scale=2 * KS, bias=-KS)
    indices(0)
    an_t(0)
    an_s(0)
    act(T.HN[:, 2048:2560], T.HN[:, 0:512], FK[0:1], FK[4:5])
    vcopy(T.Hf[:], T.heirI[:], ["heirI"], ["Hf"])
    row(0, "Hf", "HNh")
    ts(T.E0[:], T.e0i[:], 0, A.is_equal, ["e0i"], ["E0"])
    prep_t(0)
    ts(T.cb[:], T.maskP[:, 0:1], float(BIAS), A.mult, ["maskP"], ["cb"])
    prep_nh(0)
    ts(T.ownH[:], T.ownI[:], BIAS, A.subtract, ["ownI"], ["ownH"])
    prep_ma(0)
    ts(T.K1[:], T.BO[:, 0:128:16], 1.0, A.mult, ["BO"], ["K1"])
    act(T.K4[:], T.BO[:, 0:128:16], ["BO"], ["K4"], scale=4096.0)
    act(T.RM[:], T.BO[:, 0:128:16], ["BO"], ["RM"], scale=2.0)
    for k in range(N0):
        n_book(k)
    deeds_hit(0, 0)
    deeds_hit(0, 1)
    deeds_list(0, 0)
    deeds_list(0, 1)
    rep(0, range(0, S0), "s")
    for k in range(N0, 7):
        n_book(k)
    deeds_end(0)
    deeds_end(1)
    offs(0)
    offs(1)
    ts(T.IdH[:], T.D0[:], 0, A.is_equal, ["D0"], ["IdH"])
    ts(T.nIdH[:, 0:128], T.D0[:], 0, A.is_equal, ["D0"], ["nIdH"], -1.0, A.mult)
    ts(T.nIdH[:, 128:256], T.D0[:], 0, A.mult, ["D0"], ["nIdH"])
    ts(T.BI[:], T.D0[:], 0, A.is_equal, ["D0"], ["BI"], float(BIG), A.mult)
    ts(T.RH[:, 0:8], T.V8[:], -1, A.is_equal, ["V8"], ["RH"], -1.0, A.mult)
    for k in (1, 2):
        ts(T.RH[:, 8 * k:8 * k + 8], T.V8[:], 0, A.is_equal, ["V8"], ["RH"])
    indices(1)
    rep(0, range(S0, 16), "v")
    n_book(7)
    act(T.NS[:], b[0][0:64, :], ["b0"], ["NS"])
    row(1, "NS", "HNn")
    scatter_w(0, 0)
    scatter_w(0, 1)
    scatter_h(0, 0)
    scatter_h(0, 1)

    nxt = T.cores[(rank + 1) % n]
    prv = T.cores[(rank - 1) % n]
    for t in range(1, R):
        for ch in range(2):
            arrive("r%d%d" % (t, ch), "R%d%d" % (t, ch), prv)

    def out_yo(ch):
        loc = slice(128 * ch, 128 * ch + 128)
        turn(ch, "OT%d" % ch)
        ts(T.yof[:, loc], b[2 + ch][:, 0:128], float(BIAS), A.add, ["b%d" % (2 + ch)], ["yof%d" % ch])
        op("y", lambda: g.sync.dma_start(out=T.yo[:, loc], in_=T.yof[:, loc]), ["yof%d" % ch], [], "dout", 16)

    def done(t, ch):
        if t == R - 1:
            upd(ch, "OT%d" % ch)
        else:
            dst = "SD%d%d" % (t, ch)
            upd(ch, dst)
            send(nxt, T["R%d%d" % (t + 1, ch)][:], T[dst][:], "r%d%d" % (t + 1, ch), dst)

    for t in range(R):
        last = t == R - 1
        if t:
            for ch in (0, 1):
                deeds_hit(t, ch)
                deeds_list(t, ch)
                if ch == 0:
                    offs(0)
                deeds_end(ch)
                if ch == 1:
                    offs(1)
                scatter_h(t, ch)
                scatter_w(t, ch)
        init(t, 0, 0)
        init(t, 0, 1)
        if not last:
            prep_t(t + 1)
            an_t(t + 1)
        gs(0, 0, 0, 128)
        gv(t, 0, 0, 0, 128)
        if last:
            op("y", lambda: g.sync.dma_start(out=T.yh[:], in_=T.HN[0:128:16, 0:4096]), HK, [], "dout", 16)
            op("y", lambda: g.sync.dma_start(out=T.yd[:], in_=T.W[:, 0:4096]), WK, [], "dout", 16)
        sums_h(0, 0)
        sums_m(0, 0)
        gs(0, 1, 0, SA)
        copy_h(0)
        gs(0, 1, SA, 128)
        turn(0, "Hc0")
        init(t, 1, 0)
        gv(t, 0, 1, 0, VA)
        conv(0)
        gv(t, 0, 1, VA, 128)
        sums_h(0, 1)
        sums_m(0, 1)
        gs(1, 0, 0, SB)
        copy_h(1)
        gs(1, 0, SB, 128)
        turn(1, "Hc1")
        init(t, 1, 1)
        gv(t, 1, 0, 0, VB)
        conv(1)
        gv(t, 1, 0, VB, 128)
        stay_v(0)
        first(0)
        sums_h(1, 0)
        stay_t(0)
        sums_m(1, 0)
        first_t(0)
        gs(1, 1, 0, 128)
        stay_s(1)
        gv(t, 1, 1, 0, VC)
        move(0)
        done(t, 0)
        gv(t, 1, 1, VC, 128)
        sums_h(1, 1)
        stay_t(1)
        if last:
            out_yo(0)
        sums_m(1, 1)
        first(1)
        first_t(1)
        if not last:
            prep_ma(t + 1)
            if t + 2 < R:
                indices(t + 2)
            an_s(t + 1)
            if t + 1 < n:
                rep(t + 1, range(0, RB), "s")
                rep(t + 1, range(16 - VR, 16), "v")
        move(1)
        done(t, 1)
        if last:
            out_yo(1)
        else:
            prep_nh(t + 1)
            if t + 1 < n:
                rep(t + 1, range(RB, 16 - VR), "s")

    g.sync.wait_ge(T.sem.dout, cnt["dout"])
    wait("p", {s: c for s, c in cnt.items() if s != "dout"})
